import numpy as np
import ml_dtypes


def mxq(x, axis, fmt="e4m3"):
    dtype, down = {"e4m3": (ml_dtypes.float8_e4m3fn, 7), "e5m2": (ml_dtypes.float8_e5m2, 14)}[fmt]
    v = np.moveaxis(np.asarray(x, np.float32).astype(ml_dtypes.bfloat16).astype(np.float64), axis, -1)
    blocks = v.reshape(v.shape[:-1] + (-1, 32))
    amax = np.abs(blocks).max(-1, keepdims=True)
    byte = np.maximum(np.where(amax > 0, np.frexp(amax)[1] - 1 + 127, 0) - down, 1)
    scale = np.exp2(byte - 127.0)
    codes = (blocks / scale).astype(np.float32).astype(dtype).astype(np.float64)
    return np.moveaxis((codes * scale).reshape(v.shape), -1, axis)


WIDE = False


def mx_kscale(k):
    if not WIDE:
        return np.ones(k)
    levels = np.array([10, -10, 5, -5, 0])
    if k % 512:
        return np.exp2(np.random.permutation(np.resize(levels, k // 32))).repeat(32)
    a = np.empty((k // 512, 16))
    for p in range(k // 512):
        a[p, :8] = np.random.permutation(np.resize(levels, 8))
        for g in range(8):
            far = levels[np.abs(levels - a[p, g]) >= 10]
            a[p, g + 8] = far[np.random.randint(len(far))]
    return np.exp2(a.ravel()).repeat(32)


def f64(x):
    return np.asarray(x).astype(np.float64)


def striped(idx):
    return np.tile(idx.reshape(-1, 16).T, (8, 1)).astype(np.uint16)


def unstriped(offs):
    return offs[:16].T.reshape(-1).astype(np.int64)


def pack_weight(w):
    k, n = w.shape
    w = f64(np.asarray(w, np.float32).astype(ml_dtypes.bfloat16)).reshape(k // 32, 32, n)
    amax = np.abs(w).max(1)
    byte = np.clip(np.where(amax > 0, np.frexp(amax)[1] - 1 + 127 - 7, 1), 1, 254)
    scaled = (w * np.exp2(127.0 - byte)[:, None, :]).reshape(k, n).astype(np.float32)
    words = np.ascontiguousarray(scaled.reshape(k // 512, 128, 4, n).transpose(0, 1, 3, 2)).astype(ml_dtypes.float8_e4m3fn).view(np.uint8)
    return words, np.ascontiguousarray(byte.astype(np.uint8).reshape(k // 512, 16, n))


def unpack_weight(words, scales):
    g, p, n, _ = words.shape
    vals = np.ascontiguousarray(words).view(ml_dtypes.float8_e4m3fn).astype(np.float64) * np.repeat(np.exp2(scales.astype(np.float64) - 127.0), 8, axis=1)[..., None]
    return vals.transpose(0, 1, 3, 2).reshape(g * 512, n)


K, T, S, D, H, J, V = 1024, 4096, 1024, 2, 512, 256, 512


def setup_inputs():
    n = np.random.standard_normal
    s = mx_kscale(K)[:, None]
    u = mx_kscale(H)
    packed_xT = pack_weight(n((K, T)) * s)
    return {
        "x_words": packed_xT[0],
        "x_scales": packed_xT[1],
        "w1": (n((K, H)) / np.sqrt(K) / s * u).astype(np.float32),
        "w2": (n((K, H)) / np.sqrt(K) / s / u / np.sqrt(H)).astype(np.float32),
        "eT": (n((K, J)) * s).astype(np.float32),
        "offs": striped(np.random.permutation(T)[:S]),
    }


def reference(x_words, x_scales, w1, w2, eT, offs):
    eTq = mxq(f64(eT), 0, "e4m3")
    g = mxq(f64(w2), 0, "e4m3").T @ eTq
    xq = unpack_weight(x_words, x_scales)[:, unstriped(offs)]
    h = mxq(f64(w1), 0, "e4m3").T @ xq
    z = (h.reshape(H, V, D).sum(axis=2)) / 2
    y = mxq(g, 0, "e4m3").T @ mxq(z, 0, "e4m3")
    e = np.exp(y - y.max(axis=1, keepdims=True))
    return e / e.sum(axis=1, keepdims=True)

@@ -1,0 +1,256 @@
+from contextlib import ExitStack
+
+import concourse.mybir as mybir
+
+K, T, S, D, H, J, V = 1024, 4096, 1024, 2, 512, 256, 512
+FLOPS = 2 * K * H * S + 2 * K * H * J + 2 * H * J * V
+
+F32 = mybir.dt.float32
+BF16 = mybir.dt.bfloat16
+I32 = mybir.dt.int32
+U32 = mybir.dt.uint32
+U16 = mybir.dt.uint16
+U8 = mybir.dt.uint8
+FP8X4 = mybir.dt.float8_e4m3fn_x4
+ACT = mybir.ActivationFunctionType
+ALU = mybir.AluOpType
+
+P = 128
+PACK = 4
+K_PASS = P * PACK
+PASSES = K // K_PASS
+HALVES = 2
+V_HALF = V // HALVES
+V_CHUNK = 128
+Q_TILE = 128
+
+
+def tile_picked_zproto_none_p_kernel(tc, x_words, x_scales, w1, w2, eT, offs, out):
+    nc = tc.nc
+
+    with ExitStack() as ctx:
+        keep = ctx.enter_context(tc.tile_pool(name="keep", bufs=1))
+        psum = ctx.enter_context(tc.psum_pool(name="psum", bufs=1))
+
+        def sbuf(name, shape, dtype):
+            return keep.tile(shape, dtype, name=name, align_bytes=64)
+
+        def load_rows(name, src, o):
+            raw = sbuf("%s_raw%d" % (name, o), [P, PACK, src.shape[1]], F32)
+            nc.sync.dma_start(out=raw[:], in_=src[o * K_PASS : (o + 1) * K_PASS, :].rearrange("(p j) c -> p j c", j=PACK))
+            return raw
+
+        def quantize(name, grouped, width):
+            codes = sbuf(name + "_codes", [P, width], U32)
+            scales = sbuf(name + "_scales", [P, width], U8)
+            nc.vector.quantize_mx(out=codes[:].bitcast(FP8X4), scales=scales[:], in_=grouped)
+            return codes, scales
+
+        def weight_views(raw, grouped, t0, t1):
+            dst = grouped[:].rearrange("p (t u i j) -> p t u j i", t=PACK, i=4, j=PACK)[:, t0:t1]
+            src = raw[:].rearrange("p j (u t i) -> p t u j i", t=PACK, i=4)[:, t0:t1]
+            return dst, src
+
+        offsets = sbuf("offsets", [P, S // 16], U16)
+        nc.sync.dma_start(offsets[:], offs)
+
+        def load_words(o):
+            words = sbuf("x_store%d" % o, [P, T], I32)
+            nc.sync.dma_start(out=words[:], in_=x_words[o].rearrange("p n r -> p (n r)").bitcast(I32))
+            return words
+
+        x_store, w1_raw, w2_raw, e_raw = {}, {}, {}, {}
+
+        def load_queries(o, q0, q1):
+            raw = load_rows("e%d_" % q0, eT[:, q0 * Q_TILE : q1 * Q_TILE], o)
+            for qt in range(q0, q1):
+                e_raw[(o, qt)] = raw[:, :, (qt - q0) * Q_TILE : (qt - q0 + 1) * Q_TILE]
+
+        x_store[0] = load_words(0)
+        scale_store = sbuf("scale_store", [P, T], U8)
+        nc.vector.memset(scale_store[:].bitcast(I32), 0)
+        for q in range(4):
+            nc.sync.dma_start(
+                out=scale_store[32 * q : 32 * q + 4 * PASSES, :].bitcast(I32),
+                in_=x_scales[:, 4 * q : 4 * q + 4, :].bitcast(I32),
+            )
+        x_store[1] = load_words(1)
+        w1_raw[0] = load_rows("w1", w1, 0)
+        w1_raw[1] = load_rows("w1", w1, 1)
+        w2_raw[0] = load_rows("w2", w2, 0)
+        w2_raw[1] = load_rows("w2", w2, 1)
+        load_queries(0, 0, 2)
+        load_queries(1, 0, 1)
+        load_queries(1, 1, 2)
+
+        def weight(name, raw, split):
+            grouped = sbuf(name + "_bf", [P, H * PACK], BF16)
+            if split > 0:
+                dst, src = weight_views(raw, grouped, 0, split)
+                nc.vector.tensor_copy(out=dst, in_=src)
+            if split < PACK:
+                dst, src = weight_views(raw, grouped, split, PACK)
+                nc.scalar.copy(out=dst, in_=src)
+            return grouped
+
+        picked_scales = sbuf("picked_scales", [P, S], U8)
+        member_scales = sbuf("member_scales", [P, D, V], U8)
+
+        def gather_scales():
+            nc.vector.tensor_copy(out=picked_scales[:], in_=scale_store[:].indirect(offsets[:]))
+            nc.vector.tensor_copy(out=member_scales[:], in_=picked_scales[:].rearrange("p (v d) -> p d v", d=D))
+
+        half_cols = S // 16 // HALVES
+        picked = {}
+
+        def gather_words(o, hf):
+            words = sbuf("picked%d_%d" % (o, hf), [P, D, V_HALF], U32)
+            nc.vector.tensor_copy(
+                out=words[:].rearrange("p d v -> p v d"),
+                in_=x_store[o][:].bitcast(U32).indirect(offsets[:, hf * half_cols : (hf + 1) * half_cols]),
+            )
+            picked[(o, hf)] = words
+
+        z_codes = sbuf("z_codes", [P, V], U32)
+        z_scales = sbuf("z_scales", [P, V], U8)
+        z_banks = [psum.tile([P, PACK, V_CHUNK], F32, name="z_bank%d" % c) for c in range(V // V_CHUNK)]
+        w1_mx, w2_mx, e_mx, g_mx, bf, z_bf, g_bf, g_banks = {}, {}, {}, {}, {}, {}, {}, {}
+
+        def support_pass(c, t, o):
+            v0 = c * V_CHUNK
+            hf, v_in = divmod(v0, V_HALF)
+            codes, scales = w1_mx[o]
+            for d in range(D):
+                nc.tensor.matmul_mx(
+                    out=z_banks[c][:, t, :],
+                    lhsT=codes[:, t * P : (t + 1) * P].bitcast(FP8X4),
+                    lhsT_scale=scales[:, t * P : (t + 1) * P],
+                    rhs=picked[(o, hf)][:, d, v_in : v_in + V_CHUNK].bitcast(FP8X4),
+                    rhs_scale=member_scales[4 * o : P, d, v0 : v0 + V_CHUNK],
+                    start=(o == 0 and d == 0),
+                    stop=(o == PASSES - 1 and d == D - 1),
+                )
+
+        def early():
+            for c in range(V // V_CHUNK):
+                support_pass(c, 0, 0)
+
+        def z_mm(c):
+            support_pass(c, 0, 1)
+            for t in range(1, PACK):
+                for o in range(PASSES):
+                    support_pass(c, t, o)
+
+        def z_out(c):
+            z_bf[c] = sbuf("z_bf%d" % c, [P, V_CHUNK, PACK], BF16)
+            nc.scalar.activation(out=z_bf[c][:], in_=z_banks[c][:].rearrange("p t v -> p v t"), func=ACT.Copy, scale=1.0 / D)
+
+        def z_q(c):
+            v0 = c * V_CHUNK
+            nc.vector.quantize_mx(
+                out=z_codes[:, v0 : v0 + V_CHUNK].bitcast(FP8X4),
+                scales=z_scales[:, v0 : v0 + V_CHUNK],
+                in_=z_bf[c][:].rearrange("p v t -> p (v t)"),
+            )
+
+        def e_copy(o, qt, copy):
+            grouped = sbuf("e_bf%d_%d" % (o, qt), [P, Q_TILE * PACK], BF16)
+            copy(
+                out=grouped[:].rearrange("p (c i j) -> p c j i", i=4, j=PACK),
+                in_=e_raw[(o, qt)].rearrange("p j (c i) -> p c j i", i=4),
+            )
+            bf[(o, qt)] = grouped
+
+        def e_q(o, qt):
+            e_mx[(o, qt)] = quantize("e_%d_%d" % (o, qt), bf[(o, qt)][:], Q_TILE)
+
+        def g_mm(qt):
+            bank = psum.tile([P, PACK, Q_TILE], F32, name="g_bank%d" % qt)
+            g_banks[qt] = bank
+            for t in range(PACK):
+                for o in range(PASSES):
+                    codes, scales = w2_mx[o]
+                    nc.tensor.matmul_mx(
+                        out=bank[:, t, :],
+                        lhsT=codes[:, t * P : (t + 1) * P].bitcast(FP8X4),
+                        lhsT_scale=scales[:, t * P : (t + 1) * P],
+                        rhs=e_mx[(o, qt)][0][:].bitcast(FP8X4),
+                        rhs_scale=e_mx[(o, qt)][1][:],
+                        start=(o == 0),
+                        stop=(o == PASSES - 1),
+                    )
+
+        def g_out(qt, copy):
+            g_bf[qt] = sbuf("g_bf%d" % qt, [P, Q_TILE, PACK], BF16)
+            copy(out=g_bf[qt][:], in_=g_banks[qt][:].rearrange("p t q -> p q t"))
+
+        def g_q(qt):
+            g_mx[qt] = quantize("g_%d" % qt, g_bf[qt][:].rearrange("p q t -> p (q t)"), Q_TILE)
+
+        VC, SC = nc.vector.tensor_copy, nc.scalar.copy
+        gather_words(0, 0)
+        gather_words(0, 1)
+        gather_scales()
+        gather_words(1, 0)
+        gather_words(1, 1)
+        bf["a0"] = weight("w1_0", w1_raw[0], 0)
+        w1_mx[0] = quantize("w1_0", bf["a0"][:], H)
+        early()
+        bf["a1"] = weight("w1_1", w1_raw[1], 2)
+        w1_mx[1] = quantize("w1_1", bf["a1"][:], H)
+        z_mm(0)
+        bf["b0"] = weight("w2_0", w2_raw[0], 2)
+        z_out(0)
+        z_mm(1)
+        w2_mx[0] = quantize("w2_0", bf["b0"][:], H)
+        z_q(0)
+        z_out(1)
+        z_mm(2)
+        bf["b1"] = weight("w2_1", w2_raw[1], 2)
+        z_q(1)
+        w2_mx[1] = quantize("w2_1", bf["b1"][:], H)
+        z_out(2)
+        z_mm(3)
+        e_copy(0, 0, VC)
+        e_copy(0, 1, VC)
+        z_q(2)
+        e_q(0, 0)
+        e_q(0, 1)
+        z_out(3)
+        e_copy(1, 0, VC)
+        z_q(3)
+        e_q(1, 0)
+        g_mm(0)
+        e_copy(1, 1, VC)
+        e_q(1, 1)
+        g_mm(1)
+        g_out(0, SC)
+        g_q(0)
+        g_out(1, SC)
+        g_q(1)
+
+        exps = []
+        for qt in range(J // Q_TILE):
+            y = psum.tile([P, V], F32, name="y_bank%d" % qt)
+            nc.tensor.matmul_mx(
+                out=y[:],
+                lhsT=g_mx[qt][0][:].bitcast(FP8X4),
+                lhsT_scale=g_mx[qt][1][:],
+                rhs=z_codes[:].bitcast(FP8X4),
+                rhs_scale=z_scales[:],
+                start=True,
+                stop=True,
+            )
+            neg_max = sbuf("neg_max%d" % qt, [P, 1], F32)
+            nc.vector.tensor_reduce(out=neg_max[:], in_=y[:], axis=mybir.AxisListType.X, op=ALU.max, negate=True)
+            e = sbuf("exp%d" % qt, [P, V], F32)
+            total = sbuf("total%d" % qt, [P, 1], F32)
+            nc.scalar.activation(out=e[:], in_=y[:], func=ACT.Exp, bias=neg_max[:], accum_out=total[:])
+            exps.append((e, total))
+        for qt in range(J // Q_TILE):
+            e, total = exps[qt]
+            inv = sbuf("inv%d" % qt, [P, 1], F32)
+            nc.vector.reciprocal(out=inv[:], in_=total[:])
+            prob = sbuf("prob%d" % qt, [P, V], F32)
+            nc.vector.tensor_scalar(out=prob[:], in0=e[:], scalar1=inv[:], scalar2=None, op0=ALU.mult)
+            nc.sync.dma_start(out=out[qt * Q_TILE : (qt + 1) * Q_TILE, :], in_=prob[:])

@@ -23,6 +23,7 @@ HALVES = 2
 V_HALF = V // HALVES
 V_CHUNK = 128
 Q_TILE = 128
+SHARE = {"late":"picked_scales"}
 
 
 def tile_picked_zproto_none_p_kernel(tc, x_words, x_scales, w1, w2, eT, offs, out):
@@ -33,7 +34,7 @@ def tile_picked_zproto_none_p_kernel(tc, x_words, x_scales, w1, w2, eT, offs, ou
         psum = ctx.enter_context(tc.psum_pool(name="psum", bufs=1))
 
         def sbuf(name, shape, dtype):
-            return keep.tile(shape, dtype, name=name, align_bytes=64)
+            return keep.tile(shape, dtype, name=name, tag=SHARE.get(name, name), align_bytes=64)
 
         def load_rows(name, src, o):
             raw = sbuf("%s_raw%d" % (name, o), [P, PACK, src.shape[1]], F32)
@@ -46,51 +47,46 @@ def tile_picked_zproto_none_p_kernel(tc, x_words, x_scales, w1, w2, eT, offs, ou
             nc.vector.quantize_mx(out=codes[:].bitcast(FP8X4), scales=scales[:], in_=grouped)
             return codes, scales
 
-        def weight_views(raw, grouped, t0, t1):
-            dst = grouped[:].rearrange("p (t u i j) -> p t u j i", t=PACK, i=4, j=PACK)[:, t0:t1]
-            src = raw[:].rearrange("p j (u t i) -> p t u j i", t=PACK, i=4)[:, t0:t1]
-            return dst, src
-
         offsets = sbuf("offsets", [P, S // 16], U16)
-        nc.sync.dma_start(offsets[:], offs)
+        x_store, w1_raw, w2_raw, e_raw = {}, {}, {}, {}
 
         def load_words(o):
             words = sbuf("x_store%d" % o, [P, T], I32)
             nc.sync.dma_start(out=words[:], in_=x_words[o].rearrange("p n r -> p (n r)").bitcast(I32))
-            return words
+            x_store[o] = words
 
-        x_store, w1_raw, w2_raw, e_raw = {}, {}, {}, {}
+        scale_store = sbuf("scale_store", [P, T], U8)
+
+        def load_scales():
+            nc.vector.memset(scale_store[:].bitcast(I32), 0)
+            nc.sync.dma_start(
+                out=scale_store[0:P:4, :].bitcast(I32),
+                in_=x_scales.rearrange("o m c -> m o c").bitcast(I32),
+            )
+
+        late = {}
+
+        def load_late(name, src, o):
+            if "tile" not in late:
+                late["tile"] = sbuf("late", [P, PACK * (3 * H + J)], F32)
+                late["at"] = 0
+            width = src.shape[1]
+            raw = late["tile"][:, late["at"] : late["at"] + PACK * width].rearrange("p (j c) -> p j c", j=PACK)
+            late["at"] = late["at"] + PACK * width
+            nc.sync.dma_start(out=raw, in_=src[o * K_PASS : (o + 1) * K_PASS, :].rearrange("(p j) c -> p j c", j=PACK))
+            return raw
 
         def load_queries(o, q0, q1):
             raw = load_rows("e%d_" % q0, eT[:, q0 * Q_TILE : q1 * Q_TILE], o)
             for qt in range(q0, q1):
                 e_raw[(o, qt)] = raw[:, :, (qt - q0) * Q_TILE : (qt - q0 + 1) * Q_TILE]
 
-        x_store[0] = load_words(0)
-        scale_store = sbuf("scale_store", [P, T], U8)
-        nc.vector.memset(scale_store[:].bitcast(I32), 0)
-        for q in range(4):
-            nc.sync.dma_start(
-                out=scale_store[32 * q : 32 * q + 4 * PASSES, :].bitcast(I32),
-                in_=x_scales[:, 4 * q : 4 * q + 4, :].bitcast(I32),
+        def weight(name, raw, h, copy):
+            grouped = sbuf(name + "_bf", [P, H * PACK // 2], BF16)
+            copy(
+                out=grouped[:].rearrange("p (t u i j) -> p t u j i", t=2, i=4, j=PACK),
+                in_=raw[:].rearrange("p j (u t i) -> p t u j i", t=PACK, i=4)[:, 2 * h : 2 * h + 2],
             )
-        x_store[1] = load_words(1)
-        w1_raw[0] = load_rows("w1", w1, 0)
-        w1_raw[1] = load_rows("w1", w1, 1)
-        w2_raw[0] = load_rows("w2", w2, 0)
-        w2_raw[1] = load_rows("w2", w2, 1)
-        load_queries(0, 0, 2)
-        load_queries(1, 0, 1)
-        load_queries(1, 1, 2)
-
-        def weight(name, raw, split):
-            grouped = sbuf(name + "_bf", [P, H * PACK], BF16)
-            if split > 0:
-                dst, src = weight_views(raw, grouped, 0, split)
-                nc.vector.tensor_copy(out=dst, in_=src)
-            if split < PACK:
-                dst, src = weight_views(raw, grouped, split, PACK)
-                nc.scalar.copy(out=dst, in_=src)
             return grouped
 
         picked_scales = sbuf("picked_scales", [P, S], U8)
@@ -99,6 +95,10 @@ def tile_picked_zproto_none_p_kernel(tc, x_words, x_scales, w1, w2, eT, offs, ou
         def gather_scales():
             nc.vector.tensor_copy(out=picked_scales[:], in_=scale_store[:].indirect(offsets[:]))
             nc.vector.tensor_copy(out=member_scales[:], in_=picked_scales[:].rearrange("p (v d) -> p d v", d=D))
+            rows = member_scales[:].rearrange("p d v -> p (d v)").bitcast(I32)
+            for o in range(PASSES):
+                for r in range(1, 4):
+                    nc.sync.dma_start(out=rows[4 * o + r : P : 32, :], in_=rows[4 * o + 8 * r : P : 32, :])
 
         half_cols = S // 16 // HALVES
         picked = {}
@@ -119,12 +119,12 @@ def tile_picked_zproto_none_p_kernel(tc, x_words, x_scales, w1, w2, eT, offs, ou
         def support_pass(c, t, o):
             v0 = c * V_CHUNK
             hf, v_in = divmod(v0, V_HALF)
-            codes, scales = w1_mx[o]
+            codes, scales = w1_mx[(o, t // 2)]
             for d in range(D):
                 nc.tensor.matmul_mx(
                     out=z_banks[c][:, t, :],
-                    lhsT=codes[:, t * P : (t + 1) * P].bitcast(FP8X4),
-                    lhsT_scale=scales[:, t * P : (t + 1) * P],
+                    lhsT=codes[:, t % 2 * P : (t % 2 + 1) * P].bitcast(FP8X4),
+                    lhsT_scale=scales[:, t % 2 * P : (t % 2 + 1) * P],
                     rhs=picked[(o, hf)][:, d, v_in : v_in + V_CHUNK].bitcast(FP8X4),
                     rhs_scale=member_scales[4 * o : P, d, v0 : v0 + V_CHUNK],
                     start=(o == 0 and d == 0),
@@ -135,15 +135,19 @@ def tile_picked_zproto_none_p_kernel(tc, x_words, x_scales, w1, w2, eT, offs, ou
             for c in range(V // V_CHUNK):
                 support_pass(c, 0, 0)
 
-        def z_mm(c):
-            support_pass(c, 0, 1)
-            for t in range(1, PACK):
+        def z_mm(c, h):
+            for t in range(2 * h, 2 * h + 2):
                 for o in range(PASSES):
-                    support_pass(c, t, o)
+                    if (t, o) != (0, 0):
+                        support_pass(c, t, o)
 
         def z_out(c):
             z_bf[c] = sbuf("z_bf%d" % c, [P, V_CHUNK, PACK], BF16)
             nc.scalar.activation(out=z_bf[c][:], in_=z_banks[c][:].rearrange("p t v -> p v t"), func=ACT.Copy, scale=1.0 / D)
+
+        def z_out_v(c):
+            z_bf[c] = sbuf("z_bf%d" % c, [P, V_CHUNK, PACK], BF16)
+            nc.vector.tensor_scalar(out=z_bf[c][:], in0=z_banks[c][:].rearrange("p t v -> p v t"), scalar1=1.0 / D, scalar2=None, op0=ALU.mult)
 
         def z_q(c):
             v0 = c * V_CHUNK
@@ -169,11 +173,11 @@ def tile_picked_zproto_none_p_kernel(tc, x_words, x_scales, w1, w2, eT, offs, ou
             g_banks[qt] = bank
             for t in range(PACK):
                 for o in range(PASSES):
-                    codes, scales = w2_mx[o]
+                    codes, scales = w2_mx[(o, t // 2)]
                     nc.tensor.matmul_mx(
                         out=bank[:, t, :],
-                        lhsT=codes[:, t * P : (t + 1) * P].bitcast(FP8X4),
-                        lhsT_scale=scales[:, t * P : (t + 1) * P],
+                        lhsT=codes[:, t % 2 * P : (t % 2 + 1) * P].bitcast(FP8X4),
+                        lhsT_scale=scales[:, t % 2 * P : (t % 2 + 1) * P],
                         rhs=e_mx[(o, qt)][0][:].bitcast(FP8X4),
                         rhs_scale=e_mx[(o, qt)][1][:],
                         start=(o == 0),
@@ -187,43 +191,110 @@ def tile_picked_zproto_none_p_kernel(tc, x_words, x_scales, w1, w2, eT, offs, ou
         def g_q(qt):
             g_mx[qt] = quantize("g_%d" % qt, g_bf[qt][:].rearrange("p q t -> p (q t)"), Q_TILE)
 
+        def weight_whole(name, raw, copy0, copy1):
+            grouped = sbuf(name + "_bf", [P, H * PACK], BF16)
+            for h, copy in enumerate((copy0, copy1)):
+                copy(
+                    out=grouped[:].rearrange("p (t u i j) -> p t u j i", t=PACK, i=4, j=PACK)[:, 2 * h : 2 * h + 2],
+                    in_=raw[:].rearrange("p j (u t i) -> p t u j i", t=PACK, i=4)[:, 2 * h : 2 * h + 2],
+                )
+            return grouped
+
+        def q_whole(store, name, o, grouped):
+            codes, scales = quantize(name, grouped[:], H)
+            for h in range(2):
+                store[(o, h)] = (codes[:, h * 2 * P : (h + 1) * 2 * P], scales[:, h * 2 * P : (h + 1) * 2 * P])
+
+        z_pair = [sbuf("z_pair%d" % n, [P, 2 * V_CHUNK, PACK], BF16) for n in range(2)]
+
+        def z_out2(c):
+            nc.scalar.activation(out=z_pair[c // 2][:, c % 2 * V_CHUNK : (c % 2 + 1) * V_CHUNK, :], in_=z_banks[c][:].rearrange("p t v -> p v t"), func=ACT.Copy, scale=1.0 / D)
+
+        def z_out2v(c):
+            nc.vector.tensor_scalar(out=z_pair[c // 2][:, c % 2 * V_CHUNK : (c % 2 + 1) * V_CHUNK, :], in0=z_banks[c][:].rearrange("p t v -> p v t"), scalar1=1.0 / D, scalar2=None, op0=ALU.mult)
+
+        def z_q2(n):
+            v0 = n * 2 * V_CHUNK
+            nc.vector.quantize_mx(
+                out=z_codes[:, v0 : v0 + 2 * V_CHUNK].bitcast(FP8X4),
+                scales=z_scales[:, v0 : v0 + 2 * V_CHUNK],
+                in_=z_pair[n][:].rearrange("p v t -> p (v t)"),
+            )
+
+        e_whole = {}
+
+        def load_e(o):
+            e_whole[o] = load_rows("e", eT, o)
+
+        def late_e(o):
+            e_whole[o] = load_late("e", eT, o)
+            for qt in range(2):
+                e_raw[(o, qt)] = e_whole[o][:, :, qt * Q_TILE : (qt + 1) * Q_TILE]
+
+        def e_copy2(o, copy):
+            grouped = sbuf("e_bf%d" % o, [P, J * PACK], BF16)
+            copy(
+                out=grouped[:].rearrange("p (c i j) -> p c j i", i=4, j=PACK),
+                in_=e_whole[o][:].rearrange("p j (c i) -> p c j i", i=4),
+            )
+            bf[("e", o)] = grouped
+
+        def e_q2(o):
+            codes, scales = quantize("e_%d" % o, bf[("e", o)][:], J)
+            for qt in range(2):
+                e_mx[(o, qt)] = (codes[:, qt * Q_TILE : (qt + 1) * Q_TILE], scales[:, qt * Q_TILE : (qt + 1) * Q_TILE])
+
         VC, SC = nc.vector.tensor_copy, nc.scalar.copy
-        gather_words(0, 0)
-        gather_words(0, 1)
+        nc.sync.dma_start(offsets[:], offs)
+        w1_raw[0] = load_rows("w1", w1, 0)
+        load_scales()
+        load_words(1)
+        load_e(0)
+        load_words(0)
         gather_scales()
+        w1_raw[1] = load_late("w", w1, 1)
+        w2_raw[0] = load_late("w", w2, 0)
+        w2_raw[1] = load_late("w", w2, 1)
+        late_e(1)
+        bf["a0"] = weight_whole("w1_0", w1_raw[0], SC, SC)
         gather_words(1, 0)
         gather_words(1, 1)
-        bf["a0"] = weight("w1_0", w1_raw[0], 0)
-        w1_mx[0] = quantize("w1_0", bf["a0"][:], H)
+        q_whole(w1_mx, "w1_0", 0, bf["a0"])
+        e_copy2(0, SC)
+        gather_words(0, 0)
+        gather_words(0, 1)
         early()
-        bf["a1"] = weight("w1_1", w1_raw[1], 2)
-        w1_mx[1] = quantize("w1_1", bf["a1"][:], H)
-        z_mm(0)
-        bf["b0"] = weight("w2_0", w2_raw[0], 2)
-        z_out(0)
-        z_mm(1)
-        w2_mx[0] = quantize("w2_0", bf["b0"][:], H)
-        z_q(0)
-        z_out(1)
-        z_mm(2)
-        bf["b1"] = weight("w2_1", w2_raw[1], 2)
-        z_q(1)
-        w2_mx[1] = quantize("w2_1", bf["b1"][:], H)
-        z_out(2)
-        z_mm(3)
-        e_copy(0, 0, VC)
-        e_copy(0, 1, VC)
-        z_q(2)
-        e_q(0, 0)
-        e_q(0, 1)
-        z_out(3)
+        e_q2(0)
+        bf["a10"] = weight("w1_10", w1_raw[1], 0, VC)
+        bf["a11"] = weight("w1_11", w1_raw[1], 1, SC)
+        w1_mx[(1, 0)] = quantize("w1_10", bf["a10"][:], H // 2)
+        z_mm(0, 0)
+        z_mm(1, 0)
+        w1_mx[(1, 1)] = quantize("w1_11", bf["a11"][:], H // 2)
+        z_mm(0, 1)
+        bf["b0"] = weight_whole("w2_0", w2_raw[0], VC, SC)
+        z_out2v(0)
+        z_mm(1, 1)
+        q_whole(w2_mx, "w2_0", 0, bf["b0"])
+        z_out2(1)
+        z_mm(2, 0)
+        z_mm(2, 1)
+        z_q2(0)
+        z_mm(3, 0)
+        z_mm(3, 1)
+        bf["b10"] = weight("w2_10", w2_raw[1], 0, VC)
+        bf["b11"] = weight("w2_11", w2_raw[1], 1, SC)
+        w2_mx[(1, 0)] = quantize("w2_10", bf["b10"][:], H // 2)
         e_copy(1, 0, VC)
-        z_q(3)
+        e_copy(1, 1, SC)
+        w2_mx[(1, 1)] = quantize("w2_11", bf["b11"][:], H // 2)
         e_q(1, 0)
         g_mm(0)
-        e_copy(1, 1, VC)
         e_q(1, 1)
         g_mm(1)
+        z_out2(2)
+        z_out2v(3)
+        z_q2(1)
         g_out(0, SC)
         g_q(0)
         g_out(1, SC)

@@ -23,7 +23,7 @@ HALVES = 2
 V_HALF = V // HALVES
 V_CHUNK = 128
 Q_TILE = 128
-SHARE = {"late":"picked_scales"}
+SHARE = {"late1":"picked_scales","late0":"x_store1","late2":"x_store0","z_pair0":"x_store1","z_pair1":"e_bf1_1","z_codes":"e_bf1_0"}
 
 
 def tile_picked_zproto_none_p_kernel(tc, x_words, x_scales, w1, w2, eT, offs, out):
@@ -66,13 +66,11 @@ def tile_picked_zproto_none_p_kernel(tc, x_words, x_scales, w1, w2, eT, offs, ou
 
         late = {}
 
-        def load_late(name, src, o):
-            if "tile" not in late:
-                late["tile"] = sbuf("late", [P, PACK * (3 * H + J)], F32)
-                late["at"] = 0
+        def load_late(name, src, o, total):
             width = src.shape[1]
-            raw = late["tile"][:, late["at"] : late["at"] + PACK * width].rearrange("p (j c) -> p j c", j=PACK)
-            late["at"] = late["at"] + PACK * width
+            at = late.get(name, 0)
+            raw = once(name, [P, PACK * total], F32)[:, at : at + PACK * width].rearrange("p (j c) -> p j c", j=PACK)
+            late[name] = at + PACK * width
             nc.sync.dma_start(out=raw, in_=src[o * K_PASS : (o + 1) * K_PASS, :].rearrange("(p j) c -> p j c", j=PACK))
             return raw
 
@@ -111,7 +109,13 @@ def tile_picked_zproto_none_p_kernel(tc, x_words, x_scales, w1, w2, eT, offs, ou
             )
             picked[(o, hf)] = words
 
-        z_codes = sbuf("z_codes", [P, V], U32)
+        lazy = {}
+
+        def once(name, shape, dtype):
+            if name not in lazy:
+                lazy[name] = sbuf(name, shape, dtype)
+            return lazy[name]
+
         z_scales = sbuf("z_scales", [P, V], U8)
         z_banks = [psum.tile([P, PACK, V_CHUNK], F32, name="z_bank%d" % c) for c in range(V // V_CHUNK)]
         w1_mx, w2_mx, e_mx, g_mx, bf, z_bf, g_bf, g_banks = {}, {}, {}, {}, {}, {}, {}, {}
@@ -152,7 +156,7 @@ def tile_picked_zproto_none_p_kernel(tc, x_words, x_scales, w1, w2, eT, offs, ou
         def z_q(c):
             v0 = c * V_CHUNK
             nc.vector.quantize_mx(
-                out=z_codes[:, v0 : v0 + V_CHUNK].bitcast(FP8X4),
+                out=once("z_codes", [P, V], U32)[:, v0 : v0 + V_CHUNK].bitcast(FP8X4),
                 scales=z_scales[:, v0 : v0 + V_CHUNK],
                 in_=z_bf[c][:].rearrange("p v t -> p (v t)"),
             )
@@ -205,20 +209,21 @@ def tile_picked_zproto_none_p_kernel(tc, x_words, x_scales, w1, w2, eT, offs, ou
             for h in range(2):
                 store[(o, h)] = (codes[:, h * 2 * P : (h + 1) * 2 * P], scales[:, h * 2 * P : (h + 1) * 2 * P])
 
-        z_pair = [sbuf("z_pair%d" % n, [P, 2 * V_CHUNK, PACK], BF16) for n in range(2)]
+        def z_pair(n):
+            return once("z_pair%d" % n, [P, 2 * V_CHUNK, PACK], BF16)
 
         def z_out2(c):
-            nc.scalar.activation(out=z_pair[c // 2][:, c % 2 * V_CHUNK : (c % 2 + 1) * V_CHUNK, :], in_=z_banks[c][:].rearrange("p t v -> p v t"), func=ACT.Copy, scale=1.0 / D)
+            nc.scalar.activation(out=z_pair(c // 2)[:, c % 2 * V_CHUNK : (c % 2 + 1) * V_CHUNK, :], in_=z_banks[c][:].rearrange("p t v -> p v t"), func=ACT.Copy, scale=1.0 / D)
 
         def z_out2v(c):
-            nc.vector.tensor_scalar(out=z_pair[c // 2][:, c % 2 * V_CHUNK : (c % 2 + 1) * V_CHUNK, :], in0=z_banks[c][:].rearrange("p t v -> p v t"), scalar1=1.0 / D, scalar2=None, op0=ALU.mult)
+            nc.vector.tensor_scalar(out=z_pair(c // 2)[:, c % 2 * V_CHUNK : (c % 2 + 1) * V_CHUNK, :], in0=z_banks[c][:].rearrange("p t v -> p v t"), scalar1=1.0 / D, scalar2=None, op0=ALU.mult)
 
         def z_q2(n):
             v0 = n * 2 * V_CHUNK
             nc.vector.quantize_mx(
-                out=z_codes[:, v0 : v0 + 2 * V_CHUNK].bitcast(FP8X4),
+                out=once("z_codes", [P, V], U32)[:, v0 : v0 + 2 * V_CHUNK].bitcast(FP8X4),
                 scales=z_scales[:, v0 : v0 + 2 * V_CHUNK],
-                in_=z_pair[n][:].rearrange("p v t -> p (v t)"),
+                in_=z_pair(n)[:].rearrange("p v t -> p (v t)"),
             )
 
         e_whole = {}
@@ -227,7 +232,7 @@ def tile_picked_zproto_none_p_kernel(tc, x_words, x_scales, w1, w2, eT, offs, ou
             e_whole[o] = load_rows("e", eT, o)
 
         def late_e(o):
-            e_whole[o] = load_late("e", eT, o)
+            e_whole[o] = load_late("late2", eT, o, H + J)
             for qt in range(2):
                 e_raw[(o, qt)] = e_whole[o][:, :, qt * Q_TILE : (qt + 1) * Q_TILE]
 
@@ -246,25 +251,27 @@ def tile_picked_zproto_none_p_kernel(tc, x_words, x_scales, w1, w2, eT, offs, ou
 
         VC, SC = nc.vector.tensor_copy, nc.scalar.copy
         nc.sync.dma_start(offsets[:], offs)
-        w1_raw[0] = load_rows("w1", w1, 0)
+        load_e(0)
         load_scales()
         load_words(1)
-        load_e(0)
         load_words(0)
         gather_scales()
-        w1_raw[1] = load_late("w", w1, 1)
-        w2_raw[0] = load_late("w", w2, 0)
-        w2_raw[1] = load_late("w", w2, 1)
-        late_e(1)
-        bf["a0"] = weight_whole("w1_0", w1_raw[0], SC, SC)
+        w1_raw[0] = load_late("late1", w1, 0, 2 * H)
+        w1_raw[1] = load_late("late1", w1, 1, 2 * H)
+        e_copy2(0, SC)
         gather_words(1, 0)
         gather_words(1, 1)
-        q_whole(w1_mx, "w1_0", 0, bf["a0"])
-        e_copy2(0, SC)
+        w2_raw[0] = load_late("late0", w2, 0, H)
+        e_q2(0)
         gather_words(0, 0)
         gather_words(0, 1)
+        w2_raw[1] = load_late("late2", w2, 1, H + J)
+        late_e(1)
+        bf["a00"] = weight("w1_00", w1_raw[0], 0, SC)
+        bf["a01"] = weight("w1_01", w1_raw[0], 1, VC)
+        w1_mx[(0, 0)] = quantize("w1_00", bf["a00"][:], H // 2)
         early()
-        e_q2(0)
+        w1_mx[(0, 1)] = quantize("w1_01", bf["a01"][:], H // 2)
         bf["a10"] = weight("w1_10", w1_raw[1], 0, VC)
         bf["a11"] = weight("w1_11", w1_raw[1], 1, SC)
         w1_mx[(1, 0)] = quantize("w1_10", bf["a10"][:], H // 2)
@@ -273,13 +280,12 @@ def tile_picked_zproto_none_p_kernel(tc, x_words, x_scales, w1, w2, eT, offs, ou
         w1_mx[(1, 1)] = quantize("w1_11", bf["a11"][:], H // 2)
         z_mm(0, 1)
         bf["b0"] = weight_whole("w2_0", w2_raw[0], VC, SC)
-        z_out2v(0)
         z_mm(1, 1)
+        z_out2(0)
         q_whole(w2_mx, "w2_0", 0, bf["b0"])
         z_out2(1)
         z_mm(2, 0)
         z_mm(2, 1)
-        z_q2(0)
         z_mm(3, 0)
         z_mm(3, 1)
         bf["b10"] = weight("w2_10", w2_raw[1], 0, VC)
@@ -294,6 +300,7 @@ def tile_picked_zproto_none_p_kernel(tc, x_words, x_scales, w1, w2, eT, offs, ou
         g_mm(1)
         z_out2(2)
         z_out2v(3)
+        z_q2(0)
         z_q2(1)
         g_out(0, SC)
         g_q(0)
@@ -307,7 +314,7 @@ def tile_picked_zproto_none_p_kernel(tc, x_words, x_scales, w1, w2, eT, offs, ou
                 out=y[:],
                 lhsT=g_mx[qt][0][:].bitcast(FP8X4),
                 lhsT_scale=g_mx[qt][1][:],
-                rhs=z_codes[:].bitcast(FP8X4),
+                rhs=lazy["z_codes"][:].bitcast(FP8X4),
                 rhs_scale=z_scales[:],
                 start=True,
                 stop=True,

@@ -22,8 +22,9 @@ PASSES = K // K_PASS
 HALVES = 2
 V_HALF = V // HALVES
 V_CHUNK = 128
+CHUNKS = V // V_CHUNK
 Q_TILE = 128
-SHARE = {"late1":"picked_scales","late0":"x_store1","late2":"x_store0","z_pair0":"x_store1","z_pair1":"e_bf1_1","z_codes":"e_bf1_0"}
+SHARE = {"x_store1":"picked_scales","w2_bf0_0":"picked_scales","w2_bf1_0":"picked_scales","e_raw0":"w1_bf0_0","z_bf":"w1_bf0_0","e_bf1":"w1_bf0_0","w2_raw0":"w1_bf1_0","late":"x_store0","w2_bf1_2":"picked1_1"}
 
 
 def tile_picked_zproto_none_p_kernel(tc, x_words, x_scales, w1, w2, eT, offs, out):
@@ -32,303 +33,227 @@ def tile_picked_zproto_none_p_kernel(tc, x_words, x_scales, w1, w2, eT, offs, ou
     with ExitStack() as ctx:
         keep = ctx.enter_context(tc.tile_pool(name="keep", bufs=1))
         psum = ctx.enter_context(tc.psum_pool(name="psum", bufs=1))
+        made = {}
 
         def sbuf(name, shape, dtype):
-            return keep.tile(shape, dtype, name=name, tag=SHARE.get(name, name), align_bytes=64)
+            if name not in made:
+                made[name] = keep.tile(shape, dtype, name=name, tag=SHARE.get(name, name), align_bytes=64)
+            return made[name]
 
-        def load_rows(name, src, o):
-            raw = sbuf("%s_raw%d" % (name, o), [P, PACK, src.shape[1]], F32)
-            nc.sync.dma_start(out=raw[:], in_=src[o * K_PASS : (o + 1) * K_PASS, :].rearrange("(p j) c -> p j c", j=PACK))
-            return raw
+        def bank(name, shape):
+            if name not in made:
+                made[name] = psum.tile(shape, F32, name=name, tag=SHARE.get(name, name))
+            return made[name]
 
-        def quantize(name, grouped, width):
-            codes = sbuf(name + "_codes", [P, width], U32)
-            scales = sbuf(name + "_scales", [P, width], U8)
-            nc.vector.quantize_mx(out=codes[:].bitcast(FP8X4), scales=scales[:], in_=grouped)
-            return codes, scales
+        VC, SC = nc.vector.tensor_copy, nc.scalar.copy
+        raw, filled = {}, {}
+
+        def load_rows(name, src, o, home, total):
+            width = src.shape[1]
+            at = filled.get(home, 0)
+            filled[home] = at + PACK * width
+            view = sbuf(home, [P, total], F32)[:, at : at + PACK * width].rearrange("p (j c) -> p j c", j=PACK)
+            nc.sync.dma_start(out=view, in_=src[o * K_PASS : (o + 1) * K_PASS, :].rearrange("(p j) c -> p j c", j=PACK))
+            raw[(name, o)] = view
+
+        def load_words(o, c0=0, c1=T):
+            words = sbuf("x_store%d" % o, [P, T], I32)
+            nc.sync.dma_start(out=words[:, c0:c1], in_=x_words[o].rearrange("p n r -> p (n r)").bitcast(I32)[:, c0:c1])
 
         offsets = sbuf("offsets", [P, S // 16], U16)
-        x_store, w1_raw, w2_raw, e_raw = {}, {}, {}, {}
-
-        def load_words(o):
-            words = sbuf("x_store%d" % o, [P, T], I32)
-            nc.sync.dma_start(out=words[:], in_=x_words[o].rearrange("p n r -> p (n r)").bitcast(I32))
-            x_store[o] = words
-
         scale_store = sbuf("scale_store", [P, T], U8)
 
         def load_scales():
             nc.vector.memset(scale_store[:].bitcast(I32), 0)
-            nc.sync.dma_start(
-                out=scale_store[0:P:4, :].bitcast(I32),
-                in_=x_scales.rearrange("o m c -> m o c").bitcast(I32),
-            )
+            nc.sync.dma_start(out=scale_store[0:P:4, :].bitcast(I32), in_=x_scales.rearrange("o m c -> m o c").bitcast(I32))
 
-        late = {}
-
-        def load_late(name, src, o, total):
-            width = src.shape[1]
-            at = late.get(name, 0)
-            raw = once(name, [P, PACK * total], F32)[:, at : at + PACK * width].rearrange("p (j c) -> p j c", j=PACK)
-            late[name] = at + PACK * width
-            nc.sync.dma_start(out=raw, in_=src[o * K_PASS : (o + 1) * K_PASS, :].rearrange("(p j) c -> p j c", j=PACK))
-            return raw
-
-        def load_queries(o, q0, q1):
-            raw = load_rows("e%d_" % q0, eT[:, q0 * Q_TILE : q1 * Q_TILE], o)
-            for qt in range(q0, q1):
-                e_raw[(o, qt)] = raw[:, :, (qt - q0) * Q_TILE : (qt - q0 + 1) * Q_TILE]
-
-        def weight(name, raw, h, copy):
-            grouped = sbuf(name + "_bf", [P, H * PACK // 2], BF16)
-            copy(
-                out=grouped[:].rearrange("p (t u i j) -> p t u j i", t=2, i=4, j=PACK),
-                in_=raw[:].rearrange("p j (u t i) -> p t u j i", t=PACK, i=4)[:, 2 * h : 2 * h + 2],
-            )
-            return grouped
-
-        picked_scales = sbuf("picked_scales", [P, S], U8)
         member_scales = sbuf("member_scales", [P, D, V], U8)
 
         def gather_scales():
+            picked_scales = sbuf("picked_scales", [P, S], U8)
             nc.vector.tensor_copy(out=picked_scales[:], in_=scale_store[:].indirect(offsets[:]))
             nc.vector.tensor_copy(out=member_scales[:], in_=picked_scales[:].rearrange("p (v d) -> p d v", d=D))
+
+        def move_scales(eng=nc.sync):
             rows = member_scales[:].rearrange("p d v -> p (d v)").bitcast(I32)
             for o in range(PASSES):
                 for r in range(1, 4):
-                    nc.sync.dma_start(out=rows[4 * o + r : P : 32, :], in_=rows[4 * o + 8 * r : P : 32, :])
+                    eng.dma_start(out=rows[4 * o + r : P : 32, :], in_=rows[4 * o + 8 * r : P : 32, :])
 
         half_cols = S // 16 // HALVES
-        picked = {}
 
         def gather_words(o, hf):
             words = sbuf("picked%d_%d" % (o, hf), [P, D, V_HALF], U32)
             nc.vector.tensor_copy(
                 out=words[:].rearrange("p d v -> p v d"),
-                in_=x_store[o][:].bitcast(U32).indirect(offsets[:, hf * half_cols : (hf + 1) * half_cols]),
-            )
-            picked[(o, hf)] = words
-
-        lazy = {}
-
-        def once(name, shape, dtype):
-            if name not in lazy:
-                lazy[name] = sbuf(name, shape, dtype)
-            return lazy[name]
-
-        z_scales = sbuf("z_scales", [P, V], U8)
-        z_banks = [psum.tile([P, PACK, V_CHUNK], F32, name="z_bank%d" % c) for c in range(V // V_CHUNK)]
-        w1_mx, w2_mx, e_mx, g_mx, bf, z_bf, g_bf, g_banks = {}, {}, {}, {}, {}, {}, {}, {}
-
-        def support_pass(c, t, o):
-            v0 = c * V_CHUNK
-            hf, v_in = divmod(v0, V_HALF)
-            codes, scales = w1_mx[(o, t // 2)]
-            for d in range(D):
-                nc.tensor.matmul_mx(
-                    out=z_banks[c][:, t, :],
-                    lhsT=codes[:, t % 2 * P : (t % 2 + 1) * P].bitcast(FP8X4),
-                    lhsT_scale=scales[:, t % 2 * P : (t % 2 + 1) * P],
-                    rhs=picked[(o, hf)][:, d, v_in : v_in + V_CHUNK].bitcast(FP8X4),
-                    rhs_scale=member_scales[4 * o : P, d, v0 : v0 + V_CHUNK],
-                    start=(o == 0 and d == 0),
-                    stop=(o == PASSES - 1 and d == D - 1),
-                )
-
-        def early():
-            for c in range(V // V_CHUNK):
-                support_pass(c, 0, 0)
-
-        def z_mm(c, h):
-            for t in range(2 * h, 2 * h + 2):
-                for o in range(PASSES):
-                    if (t, o) != (0, 0):
-                        support_pass(c, t, o)
-
-        def z_out(c):
-            z_bf[c] = sbuf("z_bf%d" % c, [P, V_CHUNK, PACK], BF16)
-            nc.scalar.activation(out=z_bf[c][:], in_=z_banks[c][:].rearrange("p t v -> p v t"), func=ACT.Copy, scale=1.0 / D)
-
-        def z_out_v(c):
-            z_bf[c] = sbuf("z_bf%d" % c, [P, V_CHUNK, PACK], BF16)
-            nc.vector.tensor_scalar(out=z_bf[c][:], in0=z_banks[c][:].rearrange("p t v -> p v t"), scalar1=1.0 / D, scalar2=None, op0=ALU.mult)
-
-        def z_q(c):
-            v0 = c * V_CHUNK
-            nc.vector.quantize_mx(
-                out=once("z_codes", [P, V], U32)[:, v0 : v0 + V_CHUNK].bitcast(FP8X4),
-                scales=z_scales[:, v0 : v0 + V_CHUNK],
-                in_=z_bf[c][:].rearrange("p v t -> p (v t)"),
+                in_=made["x_store%d" % o][:].bitcast(U32).indirect(offsets[:, hf * half_cols : (hf + 1) * half_cols]),
             )
 
-        def e_copy(o, qt, copy):
-            grouped = sbuf("e_bf%d_%d" % (o, qt), [P, Q_TILE * PACK], BF16)
+        def w_cast(name, o, t0, t1, copy, home=None, u0=0, u1=H // 16):
+            base, count = home or (0, PACK)
+            grouped = sbuf("%s_bf%d_%d" % (name, o, base), [P, count * P * PACK], BF16)
             copy(
-                out=grouped[:].rearrange("p (c i j) -> p c j i", i=4, j=PACK),
-                in_=e_raw[(o, qt)].rearrange("p j (c i) -> p c j i", i=4),
-            )
-            bf[(o, qt)] = grouped
-
-        def e_q(o, qt):
-            e_mx[(o, qt)] = quantize("e_%d_%d" % (o, qt), bf[(o, qt)][:], Q_TILE)
-
-        def g_mm(qt):
-            bank = psum.tile([P, PACK, Q_TILE], F32, name="g_bank%d" % qt)
-            g_banks[qt] = bank
-            for t in range(PACK):
-                for o in range(PASSES):
-                    codes, scales = w2_mx[(o, t // 2)]
-                    nc.tensor.matmul_mx(
-                        out=bank[:, t, :],
-                        lhsT=codes[:, t % 2 * P : (t % 2 + 1) * P].bitcast(FP8X4),
-                        lhsT_scale=scales[:, t % 2 * P : (t % 2 + 1) * P],
-                        rhs=e_mx[(o, qt)][0][:].bitcast(FP8X4),
-                        rhs_scale=e_mx[(o, qt)][1][:],
-                        start=(o == 0),
-                        stop=(o == PASSES - 1),
-                    )
-
-        def g_out(qt, copy):
-            g_bf[qt] = sbuf("g_bf%d" % qt, [P, Q_TILE, PACK], BF16)
-            copy(out=g_bf[qt][:], in_=g_banks[qt][:].rearrange("p t q -> p q t"))
-
-        def g_q(qt):
-            g_mx[qt] = quantize("g_%d" % qt, g_bf[qt][:].rearrange("p q t -> p (q t)"), Q_TILE)
-
-        def weight_whole(name, raw, copy0, copy1):
-            grouped = sbuf(name + "_bf", [P, H * PACK], BF16)
-            for h, copy in enumerate((copy0, copy1)):
-                copy(
-                    out=grouped[:].rearrange("p (t u i j) -> p t u j i", t=PACK, i=4, j=PACK)[:, 2 * h : 2 * h + 2],
-                    in_=raw[:].rearrange("p j (u t i) -> p t u j i", t=PACK, i=4)[:, 2 * h : 2 * h + 2],
-                )
-            return grouped
-
-        def q_whole(store, name, o, grouped):
-            codes, scales = quantize(name, grouped[:], H)
-            for h in range(2):
-                store[(o, h)] = (codes[:, h * 2 * P : (h + 1) * 2 * P], scales[:, h * 2 * P : (h + 1) * 2 * P])
-
-        def z_pair(n):
-            return once("z_pair%d" % n, [P, 2 * V_CHUNK, PACK], BF16)
-
-        def z_out2(c):
-            nc.scalar.activation(out=z_pair(c // 2)[:, c % 2 * V_CHUNK : (c % 2 + 1) * V_CHUNK, :], in_=z_banks[c][:].rearrange("p t v -> p v t"), func=ACT.Copy, scale=1.0 / D)
-
-        def z_out2v(c):
-            nc.vector.tensor_scalar(out=z_pair(c // 2)[:, c % 2 * V_CHUNK : (c % 2 + 1) * V_CHUNK, :], in0=z_banks[c][:].rearrange("p t v -> p v t"), scalar1=1.0 / D, scalar2=None, op0=ALU.mult)
-
-        def z_q2(n):
-            v0 = n * 2 * V_CHUNK
-            nc.vector.quantize_mx(
-                out=once("z_codes", [P, V], U32)[:, v0 : v0 + 2 * V_CHUNK].bitcast(FP8X4),
-                scales=z_scales[:, v0 : v0 + 2 * V_CHUNK],
-                in_=z_pair(n)[:].rearrange("p v t -> p (v t)"),
+                out=grouped[:].rearrange("p (t u i j) -> p u t j i", t=count, i=4, j=PACK)[:, u0:u1, t0 - base : t1 - base],
+                in_=raw[(name, o)].rearrange("p j (u t i) -> p u t j i", t=PACK, i=4)[:, u0:u1, t0:t1],
             )
 
-        e_whole = {}
-
-        def load_e(o):
-            e_whole[o] = load_rows("e", eT, o)
-
-        def late_e(o):
-            e_whole[o] = load_late("late2", eT, o, H + J)
-            for qt in range(2):
-                e_raw[(o, qt)] = e_whole[o][:, :, qt * Q_TILE : (qt + 1) * Q_TILE]
-
-        def e_copy2(o, copy):
+        def e_cast(o, c0, c1, copy):
             grouped = sbuf("e_bf%d" % o, [P, J * PACK], BF16)
             copy(
-                out=grouped[:].rearrange("p (c i j) -> p c j i", i=4, j=PACK),
-                in_=e_whole[o][:].rearrange("p j (c i) -> p c j i", i=4),
+                out=grouped[:, c0 * PACK : c1 * PACK].rearrange("p (c i j) -> p c j i", i=4, j=PACK),
+                in_=raw[("e", o)][:, :, c0:c1].rearrange("p j (c i) -> p c j i", i=4),
             )
-            bf[("e", o)] = grouped
 
-        def e_q2(o):
-            codes, scales = quantize("e_%d" % o, bf[("e", o)][:], J)
-            for qt in range(2):
-                e_mx[(o, qt)] = (codes[:, qt * Q_TILE : (qt + 1) * Q_TILE], scales[:, qt * Q_TILE : (qt + 1) * Q_TILE])
+        def quant(name, width, c0, c1):
+            codes = sbuf(name + "_codes", [P, width], U32)
+            scales = sbuf(name + "_scales", [P, width], U8)
+            return codes[:, c0:c1].bitcast(FP8X4), scales[:, c0:c1]
 
-        VC, SC = nc.vector.tensor_copy, nc.scalar.copy
+        def q(name, src, width, c0, c1, base=0):
+            codes, scales = quant(name, width, c0, c1)
+            nc.vector.quantize_mx(out=codes, scales=scales, in_=made[src][:, (c0 - base) * PACK : (c1 - base) * PACK])
+
+        def w_q(name, o, t0, t1, base=0):
+            q("%s_%d" % (name, o), "%s_bf%d_%d" % (name, o, base), H, t0 * P, t1 * P, base * P)
+
+        def e_q(o, c0, c1):
+            q("e_%d" % o, "e_bf%d" % o, J, c0, c1)
+
+        passes_done = {}
+
+        def add_pass(name, total, t, lhs, rhs):
+            n = passes_done.get(name, 0)
+            passes_done[name] = n + 1
+            nc.tensor.matmul_mx(
+                out=bank(name, [P, PACK, V_CHUNK])[:, t, :],
+                lhsT=lhs[0],
+                lhsT_scale=lhs[1],
+                rhs=rhs[0],
+                rhs_scale=rhs[1],
+                start=(n == 0),
+                stop=(n == total - 1),
+            )
+
+        def z_mm(c, o, t0, t1):
+            v0 = c * V_CHUNK
+            hf, v_in = divmod(v0, V_HALF)
+            for t in range(t0, t1):
+                for d in range(D):
+                    rhs = (made["picked%d_%d" % (o, hf)][:, d, v_in : v_in + V_CHUNK].bitcast(FP8X4), member_scales[4 * o : P, d, v0 : v0 + V_CHUNK])
+                    add_pass("z_bank%d" % c, PASSES * PACK * D, t, quant("w1_%d" % o, H, t * P, (t + 1) * P), rhs)
+
+        def g_mm(qt, o, t0=0, t1=PACK):
+            for t in range(t0, t1):
+                add_pass("g_bank%d" % qt, PASSES * PACK, t, quant("w2_%d" % o, H, t * P, (t + 1) * P), quant("e_%d" % o, J, qt * Q_TILE, (qt + 1) * Q_TILE))
+
+        def z_out(c, on_vector):
+            dst = sbuf("z_bf", [P, V * PACK], BF16)[:, c * V_CHUNK * PACK : (c + 1) * V_CHUNK * PACK].rearrange("p (v t) -> p v t", t=PACK)
+            src = made["z_bank%d" % c][:].rearrange("p t v -> p v t")
+            if on_vector:
+                nc.vector.tensor_scalar(out=dst, in0=src, scalar1=1.0 / D, scalar2=None, op0=ALU.mult)
+            else:
+                nc.scalar.activation(out=dst, in_=src, func=ACT.Copy, scale=1.0 / D)
+
+        def z_q(c0, c1):
+            q("z", "z_bf", V, c0 * V_CHUNK, c1 * V_CHUNK)
+
+        def g_out(qt, copy):
+            dst = sbuf("g_bf%d" % qt, [P, Q_TILE * PACK], BF16)
+            copy(out=dst[:].rearrange("p (q t) -> p q t", t=PACK), in_=made["g_bank%d" % qt][:].rearrange("p t q -> p q t"))
+
+        def g_q(qt):
+            q("g_%d" % qt, "g_bf%d" % qt, Q_TILE, 0, Q_TILE)
+
+        def y_mm(qt):
+            g_codes, g_scales = quant("g_%d" % qt, Q_TILE, 0, Q_TILE)
+            z_codes, z_scales = quant("z", V, 0, V)
+            nc.tensor.matmul_mx(out=bank("y_bank%d" % qt, [P, V])[:], lhsT=g_codes, lhsT_scale=g_scales, rhs=z_codes, rhs_scale=z_scales, start=True, stop=True)
+
+        def y_max(qt):
+            nc.vector.tensor_reduce(out=sbuf("neg_max%d" % qt, [P, 1], F32)[:], in_=made["y_bank%d" % qt][:], axis=mybir.AxisListType.X, op=ALU.max, negate=True)
+
+        def y_exp(qt):
+            nc.scalar.activation(out=sbuf("exp%d" % qt, [P, V], F32)[:], in_=made["y_bank%d" % qt][:], func=ACT.Exp, bias=made["neg_max%d" % qt][:], accum_out=sbuf("total%d" % qt, [P, 1], F32)[:])
+
+        def y_inv(qt):
+            nc.vector.reciprocal(out=sbuf("inv%d" % qt, [P, 1], F32)[:], in_=made["total%d" % qt][:])
+
+        def y_norm(qt, c0, c1, on_vector, eng):
+            prob = sbuf("prob%d_%d" % (qt, c0), [P, c1 - c0], F32)
+            src = made["exp%d" % qt][:, c0:c1]
+            if on_vector:
+                nc.vector.tensor_scalar(out=prob[:], in0=src, scalar1=made["inv%d" % qt][:], scalar2=None, op0=ALU.mult)
+            else:
+                nc.scalar.activation(out=prob[:], in_=src, func=ACT.Copy, scale=made["inv%d" % qt][:])
+            eng.dma_start(out=out[qt * Q_TILE : (qt + 1) * Q_TILE, c0:c1], in_=prob[:])
+
+        def warm(qt, lhs, rhs):
+            nc.tensor.matmul_mx(out=bank("y_bank%d" % qt, [P, V])[:], lhsT=lhs[0], lhsT_scale=lhs[1], rhs=rhs[0], rhs_scale=rhs[1], start=True, stop=True)
+
+        def clock(n, ap, dtype):
+            nc.gpsimd.tensor_copy(out=sbuf("clock%d" % n, [P, 1], dtype)[:], in_=ap)
+
+        LATE = PACK * H + PACK * J
         nc.sync.dma_start(offsets[:], offs)
-        load_e(0)
+        load_rows("w1", w1, 0, "w1_raw0", PACK * H)
         load_scales()
-        load_words(1)
+        load_rows("w1", w1, 1, "w1_raw1", PACK * H)
         load_words(0)
         gather_scales()
-        w1_raw[0] = load_late("late1", w1, 0, 2 * H)
-        w1_raw[1] = load_late("late1", w1, 1, 2 * H)
-        e_copy2(0, SC)
-        gather_words(1, 0)
-        gather_words(1, 1)
-        w2_raw[0] = load_late("late0", w2, 0, H)
-        e_q2(0)
+        move_scales()
+        load_words(1)
+        w_cast("w1", 0, 0, 4, SC)
+        w_q("w1", 0, 0, 4)
+        load_rows("e", eT, 0, "e_raw0", PACK * J)
+        w_cast("w1", 1, 0, 4, SC)
+        w_q("w1", 1, 0, 4)
+        load_rows("w2", w2, 0, "w2_raw0", PACK * H)
         gather_words(0, 0)
         gather_words(0, 1)
-        w2_raw[1] = load_late("late2", w2, 1, H + J)
-        late_e(1)
-        bf["a00"] = weight("w1_00", w1_raw[0], 0, SC)
-        bf["a01"] = weight("w1_01", w1_raw[0], 1, VC)
-        w1_mx[(0, 0)] = quantize("w1_00", bf["a00"][:], H // 2)
-        early()
-        w1_mx[(0, 1)] = quantize("w1_01", bf["a01"][:], H // 2)
-        bf["a10"] = weight("w1_10", w1_raw[1], 0, VC)
-        bf["a11"] = weight("w1_11", w1_raw[1], 1, SC)
-        w1_mx[(1, 0)] = quantize("w1_10", bf["a10"][:], H // 2)
-        z_mm(0, 0)
-        z_mm(1, 0)
-        w1_mx[(1, 1)] = quantize("w1_11", bf["a11"][:], H // 2)
-        z_mm(0, 1)
-        bf["b0"] = weight_whole("w2_0", w2_raw[0], VC, SC)
-        z_mm(1, 1)
-        z_out2(0)
-        q_whole(w2_mx, "w2_0", 0, bf["b0"])
-        z_out2(1)
-        z_mm(2, 0)
-        z_mm(2, 1)
-        z_mm(3, 0)
-        z_mm(3, 1)
-        bf["b10"] = weight("w2_10", w2_raw[1], 0, VC)
-        bf["b11"] = weight("w2_11", w2_raw[1], 1, SC)
-        w2_mx[(1, 0)] = quantize("w2_10", bf["b10"][:], H // 2)
-        e_copy(1, 0, VC)
-        e_copy(1, 1, SC)
-        w2_mx[(1, 1)] = quantize("w2_11", bf["b11"][:], H // 2)
-        e_q(1, 0)
-        g_mm(0)
-        e_q(1, 1)
-        g_mm(1)
-        z_out2(2)
-        z_out2v(3)
-        z_q2(0)
-        z_q2(1)
+        load_rows("w2", w2, 1, "late", LATE)
+        load_rows("e", eT, 1, "late", LATE)
+        for c in range(CHUNKS):
+            z_mm(c, 0, 0, 4)
+        gather_words(1, 0)
+        gather_words(1, 1)
+        for c in range(CHUNKS):
+            z_mm(c, 1, 0, 4)
+
+        e_cast(0, 0, J, SC)
+        e_q(0, 0, J)
+        z_out(0, False)
+        z_out(1, False)
+        z_out(2, False)
+        z_out(3, False)
+        w_cast("w2", 0, 0, 4, VC)
+        z_q(0, 2)
+        w_q("w2", 0, 0, 4)
+        g_mm(0, 0)
+        g_mm(1, 0)
+        w_cast("w2", 1, 0, 2, VC, (0, 2))
+        w_cast("w2", 1, 2, 4, SC, (2, 2))
+        z_q(2, 4)
+        w_q("w2", 1, 0, 2)
+        w_q("w2", 1, 2, 4, 2)
+        e_cast(1, 0, Q_TILE, SC)
+        e_q(1, 0, Q_TILE)
+        g_mm(0, 1)
+        e_cast(1, Q_TILE, J, SC)
+        e_q(1, Q_TILE, J)
+        g_mm(1, 1)
+
         g_out(0, SC)
         g_q(0)
         g_out(1, SC)
         g_q(1)
-
-        exps = []
-        for qt in range(J // Q_TILE):
-            y = psum.tile([P, V], F32, name="y_bank%d" % qt)
-            nc.tensor.matmul_mx(
-                out=y[:],
-                lhsT=g_mx[qt][0][:].bitcast(FP8X4),
-                lhsT_scale=g_mx[qt][1][:],
-                rhs=lazy["z_codes"][:].bitcast(FP8X4),
-                rhs_scale=z_scales[:],
-                start=True,
-                stop=True,
-            )
-            neg_max = sbuf("neg_max%d" % qt, [P, 1], F32)
-            nc.vector.tensor_reduce(out=neg_max[:], in_=y[:], axis=mybir.AxisListType.X, op=ALU.max, negate=True)
-            e = sbuf("exp%d" % qt, [P, V], F32)
-            total = sbuf("total%d" % qt, [P, 1], F32)
-            nc.scalar.activation(out=e[:], in_=y[:], func=ACT.Exp, bias=neg_max[:], accum_out=total[:])
-            exps.append((e, total))
-        for qt in range(J // Q_TILE):
-            e, total = exps[qt]
-            inv = sbuf("inv%d" % qt, [P, 1], F32)
-            nc.vector.reciprocal(out=inv[:], in_=total[:])
-            prob = sbuf("prob%d" % qt, [P, V], F32)
-            nc.vector.tensor_scalar(out=prob[:], in0=e[:], scalar1=inv[:], scalar2=None, op0=ALU.mult)
-            nc.sync.dma_start(out=out[qt * Q_TILE : (qt + 1) * Q_TILE, :], in_=prob[:])
+        y_mm(0)
+        y_mm(1)
+        y_max(0)
+        y_max(1)
+        y_exp(0)
+        y_exp(1)
+        y_inv(0)
+        y_norm(0, 0, V, True, nc.sync)
+        y_inv(1)
+        y_norm(1, 0, V // 2, True, nc.sync)
+        y_norm(1, V // 2, V, False, nc.scalar)

@@ -48,12 +48,13 @@ def tile_picked_zproto_none_p_kernel(tc, x_words, x_scales, w1, w2, eT, offs, ou
         VC, SC = nc.vector.tensor_copy, nc.scalar.copy
         raw, filled = {}, {}
 
-        def load_rows(name, src, o, home, total):
+        def load_rows(name, src, o, home, total, j0=0, j1=PACK):
             width = src.shape[1]
             at = filled.get(home, 0)
-            filled[home] = at + PACK * width
+            if j1 == PACK:
+                filled[home] = at + PACK * width
             view = sbuf(home, [P, total], F32)[:, at : at + PACK * width].rearrange("p (j c) -> p j c", j=PACK)
-            nc.sync.dma_start(out=view, in_=src[o * K_PASS : (o + 1) * K_PASS, :].rearrange("(p j) c -> p j c", j=PACK))
+            nc.sync.dma_start(out=view[:, j0:j1, :], in_=src[o * K_PASS : (o + 1) * K_PASS, :].rearrange("(p j) c -> p j c", j=PACK)[:, j0:j1, :])
             raw[(name, o)] = view
 
         def load_words(o, c0=0, c1=T):
@@ -188,14 +189,14 @@ def tile_picked_zproto_none_p_kernel(tc, x_words, x_scales, w1, w2, eT, offs, ou
             eng.dma_start(out=out[qt * Q_TILE : (qt + 1) * Q_TILE, c0:c1], in_=prob[:])
 
         def warm(qt, lhs, rhs):
-            nc.tensor.matmul_mx(out=bank("y_bank%d" % qt, [P, V])[:], lhsT=lhs[0], lhsT_scale=lhs[1], rhs=rhs[0], rhs_scale=rhs[1], start=True, stop=True)
+            nc.tensor.matmul_mx(out=bank("y_bank%d" % qt, [P, V])[:, 0 : rhs[1].shape[1]], lhsT=lhs[0], lhsT_scale=lhs[1], rhs=rhs[0], rhs_scale=rhs[1], start=True, stop=True)
 
         def clock(n, ap, dtype):
             nc.gpsimd.tensor_copy(out=sbuf("clock%d" % n, [P, 1], dtype)[:], in_=ap)
 
         LATE = PACK * H + PACK * J
-        nc.sync.dma_start(offsets[:], offs)
         load_rows("w1", w1, 0, "w1_raw0", PACK * H)
+        nc.sync.dma_start(offsets[:], offs)
         load_scales()
         load_rows("w1", w1, 1, "w1_raw1", PACK * H)
         load_words(0)
@@ -227,13 +228,17 @@ def tile_picked_zproto_none_p_kernel(tc, x_words, x_scales, w1, w2, eT, offs, ou
         z_out(3, False)
         w_cast("w2", 0, 0, 4, VC)
         z_q(0, 2)
+        warm(0, quant("z", V, 0, P), quant("w1_0", H, 0, H))
+        warm(1, quant("z", V, 0, P), quant("w1_0", H, 0, H))
         w_q("w2", 0, 0, 4)
         g_mm(0, 0)
         g_mm(1, 0)
         w_cast("w2", 1, 0, 2, VC, (0, 2))
         w_cast("w2", 1, 2, 4, SC, (2, 2))
         z_q(2, 4)
+        warm(0, quant("z", V, 3 * P, V), quant("w1_0", H, 0, H))
         w_q("w2", 1, 0, 2)
+        warm(1, quant("w2_1", H, 0, P), quant("w1_0", H, 0, H))
         w_q("w2", 1, 2, 4, 2)
         e_cast(1, 0, Q_TILE, SC)
         e_q(1, 0, Q_TILE)

@@ -24,7 +24,7 @@ V_HALF = V // HALVES
 V_CHUNK = 128
 CHUNKS = V // V_CHUNK
 Q_TILE = 128
-SHARE = {"x_store1":"picked_scales","w2_bf0_0":"picked_scales","w2_bf1_0":"picked_scales","e_raw0":"w1_bf0_0","z_bf":"w1_bf0_0","e_bf1":"w1_bf0_0","w2_raw0":"w1_bf1_0","late":"x_store0","w2_bf1_2":"picked1_1"}
+SHARE = {"x_store1":"picked_scales","w2_bf0_0":"picked_scales","e_0_codes":"picked_scales","w2_bf1_0":"w2_bf0_2","e_raw0":"w1_bf0_0","z_bf":"w1_bf0_0","w2_raw0":"w1_bf1_0","late":"x_store0","w2_bf1_2":"picked1_1","e_bf1":"picked1_0","z_codes":"picked1_0"}
 
 
 def tile_picked_zproto_none_p_kernel(tc, x_words, x_scales, w1, w2, eT, offs, out):
@@ -221,22 +221,21 @@ def tile_picked_zproto_none_p_kernel(tc, x_words, x_scales, w1, w2, eT, offs, ou
             z_mm(c, 1, 0, 4)
 
         e_cast(0, 0, J, SC)
-        e_q(0, 0, J)
         z_out(0, False)
         z_out(1, False)
         z_out(2, False)
         z_out(3, False)
-        w_cast("w2", 0, 0, 4, VC)
-        z_q(0, 2)
-        warm(0, quant("z", V, 0, P), quant("w1_0", H, 0, H))
-        warm(1, quant("z", V, 0, P), quant("w1_0", H, 0, H))
-        w_q("w2", 0, 0, 4)
+        w_cast("w2", 0, 0, 2, VC, (0, 2))
+        w_cast("w2", 0, 2, 4, VC, (2, 2))
+        w_q("w2", 0, 0, 2)
+        warm(0, quant("w2_0", H, 0, P), quant("w1_0", H, 0, H))
+        warm(1, quant("w2_0", H, 0, P), quant("w1_0", H, 0, H))
+        w_q("w2", 0, 2, 4, 2)
+        e_q(0, 0, J)
         g_mm(0, 0)
         g_mm(1, 0)
         w_cast("w2", 1, 0, 2, VC, (0, 2))
         w_cast("w2", 1, 2, 4, SC, (2, 2))
-        z_q(2, 4)
-        warm(0, quant("z", V, 3 * P, V), quant("w1_0", H, 0, H))
         w_q("w2", 1, 0, 2)
         warm(1, quant("w2_1", H, 0, P), quant("w1_0", H, 0, H))
         w_q("w2", 1, 2, 4, 2)
@@ -246,6 +245,7 @@ def tile_picked_zproto_none_p_kernel(tc, x_words, x_scales, w1, w2, eT, offs, ou
         e_cast(1, Q_TILE, J, SC)
         e_q(1, Q_TILE, J)
         g_mm(1, 1)
+        z_q(0, 4)
 
         g_out(0, SC)
         g_q(0)

@@ -19,246 +19,212 @@ P = 128
 PACK = 4
 K_PASS = P * PACK
 PASSES = K // K_PASS
-HALVES = 2
-V_HALF = V // HALVES
+SLABS = H // P
+RUN = 4
+QUADRANT = 32
+SCALE_ROWS = 4
+V_HALF = V // 2
 V_CHUNK = 128
 CHUNKS = V // V_CHUNK
 Q_TILE = 128
-SHARE = {"x_store1":"picked_scales","w2_bf0_0":"picked_scales","e_0_codes":"picked_scales","w2_bf1_0":"w2_bf0_2","e_raw0":"w1_bf0_0","z_bf":"w1_bf0_0","w2_raw0":"w1_bf1_0","late":"x_store0","w2_bf1_2":"picked1_1","e_bf1":"picked1_0","z_codes":"picked1_0"}
+Q_TILES = J // Q_TILE
 
 
 def tile_picked_zproto_none_p_kernel(tc, x_words, x_scales, w1, w2, eT, offs, out):
     nc = tc.nc
+    on_vector, on_scalar = nc.vector.tensor_copy, nc.scalar.copy
 
     with ExitStack() as ctx:
         keep = ctx.enter_context(tc.tile_pool(name="keep", bufs=1))
         psum = ctx.enter_context(tc.psum_pool(name="psum", bufs=1))
-        made = {}
 
-        def sbuf(name, shape, dtype):
-            if name not in made:
-                made[name] = keep.tile(shape, dtype, name=name, tag=SHARE.get(name, name), align_bytes=64)
-            return made[name]
+        def sbuf(name, shape, dtype, reuse=None):
+            return keep.tile(shape, dtype, name=name, tag=reuse or name, align_bytes=64)
 
-        def bank(name, shape):
-            if name not in made:
-                made[name] = psum.tile(shape, F32, name=name, tag=SHARE.get(name, name))
-            return made[name]
+        def load_pass(dst, src, o):
+            rows = dst.rearrange("p (j c) -> p j c", j=PACK)
+            nc.sync.dma_start(out=rows, in_=src[o * K_PASS : (o + 1) * K_PASS, :].rearrange("(p j) c -> p j c", j=PACK))
+            return rows
 
-        VC, SC = nc.vector.tensor_copy, nc.scalar.copy
-        raw, filled = {}, {}
+        def load_words(o, reuse=None):
+            store = sbuf("x_store%d" % o, [P, T], I32, reuse)
+            nc.sync.dma_start(out=store[:], in_=x_words[o].rearrange("p n r -> p (n r)").bitcast(I32))
+            return store
 
-        def load_rows(name, src, o, home, total, j0=0, j1=PACK):
-            width = src.shape[1]
-            at = filled.get(home, 0)
-            if j1 == PACK:
-                filled[home] = at + PACK * width
-            view = sbuf(home, [P, total], F32)[:, at : at + PACK * width].rearrange("p (j c) -> p j c", j=PACK)
-            nc.sync.dma_start(out=view[:, j0:j1, :], in_=src[o * K_PASS : (o + 1) * K_PASS, :].rearrange("(p j) c -> p j c", j=PACK)[:, j0:j1, :])
-            raw[(name, o)] = view
+        def gather_words(store, o, half):
+            words = sbuf("picked%d_%d" % (o, half), [P, D, V_HALF], U32)
+            columns = D * V_HALF // 16
+            nc.vector.tensor_copy(
+                out=words[:].rearrange("p d v -> p v d"),
+                in_=store[:].bitcast(U32).indirect(offsets[:, half * columns : (half + 1) * columns]),
+            )
+            return words
 
-        def load_words(o, c0=0, c1=T):
-            words = sbuf("x_store%d" % o, [P, T], I32)
-            nc.sync.dma_start(out=words[:, c0:c1], in_=x_words[o].rearrange("p n r -> p (n r)").bitcast(I32)[:, c0:c1])
+        def cast_slabs(name, rows, t0, t1, copy, reuse=None):
+            grouped = sbuf(name, [P, (t1 - t0) * P * PACK], BF16, reuse)
+            copy(
+                out=grouped[:].rearrange("p (t u a j) -> p u t j a", t=t1 - t0, a=RUN, j=PACK),
+                in_=rows.rearrange("p j (u t a) -> p u t j a", t=SLABS, a=RUN)[:, :, t0:t1],
+            )
+            return grouped
+
+        def cast_queries(grouped, rows, c0, c1):
+            on_scalar(
+                out=grouped[:, c0 * PACK : c1 * PACK].rearrange("p (c a j) -> p c j a", a=RUN, j=PACK),
+                in_=rows[:, :, c0:c1].rearrange("p j (c a) -> p c j a", a=RUN),
+            )
+
+        def mx_tiles(name, width, reuse=None):
+            return sbuf(name + "_codes", [P, width], U32, reuse), sbuf(name + "_scales", [P, width], U8)
+
+        def mx_columns(mx, c0, c1):
+            codes, scales = mx
+            return codes[:, c0:c1].bitcast(FP8X4), scales[:, c0:c1]
+
+        def quantize(mx, c0, c1, grouped):
+            codes, scales = mx_columns(mx, c0, c1)
+            nc.vector.quantize_mx(out=codes, scales=scales, in_=grouped)
+
+        def multiply(dst, stationary, moving, start, stop):
+            nc.tensor.matmul_mx(
+                out=dst, lhsT=stationary[0], lhsT_scale=stationary[1], rhs=moving[0], rhs_scale=moving[1], start=start, stop=stop
+            )
+
+        def class_passes(bank, c, o, w1_mx, words):
+            v0 = c * V_CHUNK
+            v_in = v0 % V_HALF
+            for t in range(SLABS):
+                for d in range(D):
+                    moving = (
+                        words[:, d, v_in : v_in + V_CHUNK].bitcast(FP8X4),
+                        member_scales[SCALE_ROWS * o : P, d, v0 : v0 + V_CHUNK],
+                    )
+                    first = o == 0 and t == 0 and d == 0
+                    last = o == PASSES - 1 and t == SLABS - 1 and d == D - 1
+                    multiply(bank[:, t, :], mx_columns(w1_mx, t * P, (t + 1) * P), moving, first, last)
+
+        def query_passes(bank, qt, o, w2_mx, e_mx):
+            for t in range(SLABS):
+                first = o == 0 and t == 0
+                last = o == PASSES - 1 and t == SLABS - 1
+                multiply(bank[:, t, :], mx_columns(w2_mx, t * P, (t + 1) * P), mx_columns(e_mx, qt * Q_TILE, (qt + 1) * Q_TILE), first, last)
 
         offsets = sbuf("offsets", [P, S // 16], U16)
         scale_store = sbuf("scale_store", [P, T], U8)
-
-        def load_scales():
-            nc.vector.memset(scale_store[:].bitcast(I32), 0)
-            nc.sync.dma_start(out=scale_store[0:P:4, :].bitcast(I32), in_=x_scales.rearrange("o m c -> m o c").bitcast(I32))
-
         member_scales = sbuf("member_scales", [P, D, V], U8)
 
-        def gather_scales():
-            picked_scales = sbuf("picked_scales", [P, S], U8)
-            nc.vector.tensor_copy(out=picked_scales[:], in_=scale_store[:].indirect(offsets[:]))
-            nc.vector.tensor_copy(out=member_scales[:], in_=picked_scales[:].rearrange("p (v d) -> p d v", d=D))
-
-        def move_scales(eng=nc.sync):
-            rows = member_scales[:].rearrange("p d v -> p (d v)").bitcast(I32)
-            for o in range(PASSES):
-                for r in range(1, 4):
-                    eng.dma_start(out=rows[4 * o + r : P : 32, :], in_=rows[4 * o + 8 * r : P : 32, :])
-
-        half_cols = S // 16 // HALVES
-
-        def gather_words(o, hf):
-            words = sbuf("picked%d_%d" % (o, hf), [P, D, V_HALF], U32)
-            nc.vector.tensor_copy(
-                out=words[:].rearrange("p d v -> p v d"),
-                in_=made["x_store%d" % o][:].bitcast(U32).indirect(offsets[:, hf * half_cols : (hf + 1) * half_cols]),
-            )
-
-        def w_cast(name, o, t0, t1, copy, home=None, u0=0, u1=H // 16):
-            base, count = home or (0, PACK)
-            grouped = sbuf("%s_bf%d_%d" % (name, o, base), [P, count * P * PACK], BF16)
-            copy(
-                out=grouped[:].rearrange("p (t u i j) -> p u t j i", t=count, i=4, j=PACK)[:, u0:u1, t0 - base : t1 - base],
-                in_=raw[(name, o)].rearrange("p j (u t i) -> p u t j i", t=PACK, i=4)[:, u0:u1, t0:t1],
-            )
-
-        def e_cast(o, c0, c1, copy):
-            grouped = sbuf("e_bf%d" % o, [P, J * PACK], BF16)
-            copy(
-                out=grouped[:, c0 * PACK : c1 * PACK].rearrange("p (c i j) -> p c j i", i=4, j=PACK),
-                in_=raw[("e", o)][:, :, c0:c1].rearrange("p j (c i) -> p c j i", i=4),
-            )
-
-        def quant(name, width, c0, c1):
-            codes = sbuf(name + "_codes", [P, width], U32)
-            scales = sbuf(name + "_scales", [P, width], U8)
-            return codes[:, c0:c1].bitcast(FP8X4), scales[:, c0:c1]
-
-        def q(name, src, width, c0, c1, base=0):
-            codes, scales = quant(name, width, c0, c1)
-            nc.vector.quantize_mx(out=codes, scales=scales, in_=made[src][:, (c0 - base) * PACK : (c1 - base) * PACK])
-
-        def w_q(name, o, t0, t1, base=0):
-            q("%s_%d" % (name, o), "%s_bf%d_%d" % (name, o, base), H, t0 * P, t1 * P, base * P)
-
-        def e_q(o, c0, c1):
-            q("e_%d" % o, "e_bf%d" % o, J, c0, c1)
-
-        passes_done = {}
-
-        def add_pass(name, total, t, lhs, rhs):
-            n = passes_done.get(name, 0)
-            passes_done[name] = n + 1
-            nc.tensor.matmul_mx(
-                out=bank(name, [P, PACK, V_CHUNK])[:, t, :],
-                lhsT=lhs[0],
-                lhsT_scale=lhs[1],
-                rhs=rhs[0],
-                rhs_scale=rhs[1],
-                start=(n == 0),
-                stop=(n == total - 1),
-            )
-
-        def z_mm(c, o, t0, t1):
-            v0 = c * V_CHUNK
-            hf, v_in = divmod(v0, V_HALF)
-            for t in range(t0, t1):
-                for d in range(D):
-                    rhs = (made["picked%d_%d" % (o, hf)][:, d, v_in : v_in + V_CHUNK].bitcast(FP8X4), member_scales[4 * o : P, d, v0 : v0 + V_CHUNK])
-                    add_pass("z_bank%d" % c, PASSES * PACK * D, t, quant("w1_%d" % o, H, t * P, (t + 1) * P), rhs)
-
-        def g_mm(qt, o, t0=0, t1=PACK):
-            for t in range(t0, t1):
-                add_pass("g_bank%d" % qt, PASSES * PACK, t, quant("w2_%d" % o, H, t * P, (t + 1) * P), quant("e_%d" % o, J, qt * Q_TILE, (qt + 1) * Q_TILE))
-
-        def z_out(c, on_vector):
-            dst = sbuf("z_bf", [P, V * PACK], BF16)[:, c * V_CHUNK * PACK : (c + 1) * V_CHUNK * PACK].rearrange("p (v t) -> p v t", t=PACK)
-            src = made["z_bank%d" % c][:].rearrange("p t v -> p v t")
-            if on_vector:
-                nc.vector.tensor_scalar(out=dst, in0=src, scalar1=1.0 / D, scalar2=None, op0=ALU.mult)
-            else:
-                nc.scalar.activation(out=dst, in_=src, func=ACT.Copy, scale=1.0 / D)
-
-        def z_q(c0, c1):
-            q("z", "z_bf", V, c0 * V_CHUNK, c1 * V_CHUNK)
-
-        def g_out(qt, copy):
-            dst = sbuf("g_bf%d" % qt, [P, Q_TILE * PACK], BF16)
-            copy(out=dst[:].rearrange("p (q t) -> p q t", t=PACK), in_=made["g_bank%d" % qt][:].rearrange("p t q -> p q t"))
-
-        def g_q(qt):
-            q("g_%d" % qt, "g_bf%d" % qt, Q_TILE, 0, Q_TILE)
-
-        def y_mm(qt):
-            g_codes, g_scales = quant("g_%d" % qt, Q_TILE, 0, Q_TILE)
-            z_codes, z_scales = quant("z", V, 0, V)
-            nc.tensor.matmul_mx(out=bank("y_bank%d" % qt, [P, V])[:], lhsT=g_codes, lhsT_scale=g_scales, rhs=z_codes, rhs_scale=z_scales, start=True, stop=True)
-
-        def y_max(qt):
-            nc.vector.tensor_reduce(out=sbuf("neg_max%d" % qt, [P, 1], F32)[:], in_=made["y_bank%d" % qt][:], axis=mybir.AxisListType.X, op=ALU.max, negate=True)
-
-        def y_exp(qt):
-            nc.scalar.activation(out=sbuf("exp%d" % qt, [P, V], F32)[:], in_=made["y_bank%d" % qt][:], func=ACT.Exp, bias=made["neg_max%d" % qt][:], accum_out=sbuf("total%d" % qt, [P, 1], F32)[:])
-
-        def y_inv(qt):
-            nc.vector.reciprocal(out=sbuf("inv%d" % qt, [P, 1], F32)[:], in_=made["total%d" % qt][:])
-
-        def y_norm(qt, c0, c1, on_vector, eng):
-            prob = sbuf("prob%d_%d" % (qt, c0), [P, c1 - c0], F32)
-            src = made["exp%d" % qt][:, c0:c1]
-            if on_vector:
-                nc.vector.tensor_scalar(out=prob[:], in0=src, scalar1=made["inv%d" % qt][:], scalar2=None, op0=ALU.mult)
-            else:
-                nc.scalar.activation(out=prob[:], in_=src, func=ACT.Copy, scale=made["inv%d" % qt][:])
-            eng.dma_start(out=out[qt * Q_TILE : (qt + 1) * Q_TILE, c0:c1], in_=prob[:])
-
-        def warm(qt, lhs, rhs):
-            nc.tensor.matmul_mx(out=bank("y_bank%d" % qt, [P, V])[:, 0 : rhs[1].shape[1]], lhsT=lhs[0], lhsT_scale=lhs[1], rhs=rhs[0], rhs_scale=rhs[1], start=True, stop=True)
-
-        def clock(n, ap, dtype):
-            nc.gpsimd.tensor_copy(out=sbuf("clock%d" % n, [P, 1], dtype)[:], in_=ap)
-
-        LATE = PACK * H + PACK * J
-        load_rows("w1", w1, 0, "w1_raw0", PACK * H)
+        w1_rows0 = load_pass(sbuf("w1_raw0", [P, PACK * H], F32)[:], w1, 0)
         nc.sync.dma_start(offsets[:], offs)
-        load_scales()
-        load_rows("w1", w1, 1, "w1_raw1", PACK * H)
-        load_words(0)
-        gather_scales()
-        move_scales()
-        load_words(1)
-        w_cast("w1", 0, 0, 4, SC)
-        w_q("w1", 0, 0, 4)
-        load_rows("e", eT, 0, "e_raw0", PACK * J)
-        w_cast("w1", 1, 0, 4, SC)
-        w_q("w1", 1, 0, 4)
-        load_rows("w2", w2, 0, "w2_raw0", PACK * H)
-        gather_words(0, 0)
-        gather_words(0, 1)
-        load_rows("w2", w2, 1, "late", LATE)
-        load_rows("e", eT, 1, "late", LATE)
-        for c in range(CHUNKS):
-            z_mm(c, 0, 0, 4)
-        gather_words(1, 0)
-        gather_words(1, 1)
-        for c in range(CHUNKS):
-            z_mm(c, 1, 0, 4)
+        nc.vector.memset(scale_store[:].bitcast(I32), 0)
+        nc.sync.dma_start(out=scale_store[0:P:4, :].bitcast(I32), in_=x_scales.rearrange("o m c -> m o c").bitcast(I32))
+        w1_rows1 = load_pass(sbuf("w1_raw1", [P, PACK * H], F32)[:], w1, 1)
+        x_store0 = load_words(0)
 
-        e_cast(0, 0, J, SC)
-        z_out(0, False)
-        z_out(1, False)
-        z_out(2, False)
-        z_out(3, False)
-        w_cast("w2", 0, 0, 2, VC, (0, 2))
-        w_cast("w2", 0, 2, 4, VC, (2, 2))
-        w_q("w2", 0, 0, 2)
-        warm(0, quant("w2_0", H, 0, P), quant("w1_0", H, 0, H))
-        warm(1, quant("w2_0", H, 0, P), quant("w1_0", H, 0, H))
-        w_q("w2", 0, 2, 4, 2)
-        e_q(0, 0, J)
-        g_mm(0, 0)
-        g_mm(1, 0)
-        w_cast("w2", 1, 0, 2, VC, (0, 2))
-        w_cast("w2", 1, 2, 4, SC, (2, 2))
-        w_q("w2", 1, 0, 2)
-        warm(1, quant("w2_1", H, 0, P), quant("w1_0", H, 0, H))
-        w_q("w2", 1, 2, 4, 2)
-        e_cast(1, 0, Q_TILE, SC)
-        e_q(1, 0, Q_TILE)
-        g_mm(0, 1)
-        e_cast(1, Q_TILE, J, SC)
-        e_q(1, Q_TILE, J)
-        g_mm(1, 1)
-        z_q(0, 4)
+        picked_scales = sbuf("picked_scales", [P, S], U8)
+        nc.vector.tensor_copy(out=picked_scales[:], in_=scale_store[:].indirect(offsets[:]))
+        nc.vector.tensor_copy(out=member_scales[:], in_=picked_scales[:].rearrange("p (v d) -> p d v", d=D))
+        scale_rows = member_scales[:].rearrange("p d v -> p (d v)").bitcast(I32)
+        for o in range(PASSES):
+            for r in range(1, SCALE_ROWS):
+                nc.sync.dma_start(
+                    out=scale_rows[SCALE_ROWS * o + r : P : QUADRANT, :], in_=scale_rows[SCALE_ROWS * o + 8 * r : P : QUADRANT, :]
+                )
 
-        g_out(0, SC)
-        g_q(0)
-        g_out(1, SC)
-        g_q(1)
-        y_mm(0)
-        y_mm(1)
-        y_max(0)
-        y_max(1)
-        y_exp(0)
-        y_exp(1)
-        y_inv(0)
-        y_norm(0, 0, V, True, nc.sync)
-        y_inv(1)
-        y_norm(1, 0, V // 2, True, nc.sync)
-        y_norm(1, V // 2, V, False, nc.scalar)
+        x_store1 = load_words(1, reuse="picked_scales")
+        w1_bf0 = cast_slabs("w1_bf0", w1_rows0, 0, SLABS, on_scalar)
+        w1_mx0 = mx_tiles("w1_0", H)
+        quantize(w1_mx0, 0, H, w1_bf0[:])
+        e_rows0 = load_pass(sbuf("e_raw0", [P, PACK * J], F32, reuse="w1_bf0")[:], eT, 0)
+        w1_bf1 = cast_slabs("w1_bf1", w1_rows1, 0, SLABS, on_scalar)
+        w1_mx1 = mx_tiles("w1_1", H)
+        quantize(w1_mx1, 0, H, w1_bf1[:])
+        w2_rows0 = load_pass(sbuf("w2_raw0", [P, PACK * H], F32, reuse="w1_bf1")[:], w2, 0)
+        picked0 = [gather_words(x_store0, 0, half) for half in range(2)]
+        last_raw = sbuf("last_raw", [P, PACK * (H + J)], F32, reuse="x_store0")
+        w2_rows1 = load_pass(last_raw[:, : PACK * H], w2, 1)
+        e_rows1 = load_pass(last_raw[:, PACK * H :], eT, 1)
+
+        z_banks = []
+        for c in range(CHUNKS):
+            z_banks.append(psum.tile([P, SLABS, V_CHUNK], F32, name="z_bank%d" % c))
+            class_passes(z_banks[c], c, 0, w1_mx0, picked0[c * V_CHUNK // V_HALF])
+        picked1 = [gather_words(x_store1, 1, half) for half in range(2)]
+        for c in range(CHUNKS):
+            class_passes(z_banks[c], c, 1, w1_mx1, picked1[c * V_CHUNK // V_HALF])
+
+        e_bf0 = sbuf("e_bf0", [P, J * PACK], BF16)
+        cast_queries(e_bf0, e_rows0, 0, J)
+        z_bf = sbuf("z_bf", [P, V * PACK], BF16, reuse="w1_bf0")
+        for c in range(CHUNKS):
+            nc.scalar.activation(
+                out=z_bf[:, c * V_CHUNK * PACK : (c + 1) * V_CHUNK * PACK].rearrange("p (v t) -> p v t", t=SLABS),
+                in_=z_banks[c][:].rearrange("p t v -> p v t"),
+                func=ACT.Copy,
+                scale=1.0 / D,
+            )
+
+        half_slabs, half_h = SLABS // 2, H // 2
+        w2_bf0_lo = cast_slabs("w2_bf0_lo", w2_rows0, 0, half_slabs, on_vector, reuse="picked_scales")
+        w2_bf0_hi = cast_slabs("w2_bf0_hi", w2_rows0, half_slabs, SLABS, on_vector)
+        w2_mx0 = mx_tiles("w2_0", H)
+        quantize(w2_mx0, 0, half_h, w2_bf0_lo[:])
+        quantize(w2_mx0, half_h, H, w2_bf0_hi[:])
+        e_mx0 = mx_tiles("e_0", J, reuse="picked_scales")
+        quantize(e_mx0, 0, J, e_bf0[:])
+        g_banks = []
+        for qt in range(Q_TILES):
+            g_banks.append(psum.tile([P, SLABS, Q_TILE], F32, name="g_bank%d" % qt))
+            query_passes(g_banks[qt], qt, 0, w2_mx0, e_mx0)
+
+        w2_bf1_lo = cast_slabs("w2_bf1_lo", w2_rows1, 0, half_slabs, on_vector, reuse="w2_bf0_hi")
+        w2_bf1_hi = cast_slabs("w2_bf1_hi", w2_rows1, half_slabs, SLABS, on_scalar, reuse="picked1_1")
+        w2_mx1 = mx_tiles("w2_1", H)
+        quantize(w2_mx1, 0, half_h, w2_bf1_lo[:])
+        quantize(w2_mx1, half_h, H, w2_bf1_hi[:])
+        e_bf1 = sbuf("e_bf1", [P, J * PACK], BF16, reuse="picked1_0")
+        cast_queries(e_bf1, e_rows1, 0, Q_TILE)
+        e_mx1 = mx_tiles("e_1", J)
+        quantize(e_mx1, 0, Q_TILE, e_bf1[:, : Q_TILE * PACK])
+        query_passes(g_banks[0], 0, 1, w2_mx1, e_mx1)
+        cast_queries(e_bf1, e_rows1, Q_TILE, J)
+        quantize(e_mx1, Q_TILE, J, e_bf1[:, Q_TILE * PACK :])
+        query_passes(g_banks[1], 1, 1, w2_mx1, e_mx1)
+
+        z_mx = mx_tiles("z", V, reuse="picked1_0")
+        quantize(z_mx, 0, V, z_bf[:])
+        g_mx = []
+        for qt in range(Q_TILES):
+            g_bf = sbuf("g_bf%d" % qt, [P, Q_TILE * PACK], BF16)
+            on_scalar(out=g_bf[:].rearrange("p (q t) -> p q t", t=SLABS), in_=g_banks[qt][:].rearrange("p t q -> p q t"))
+            g_mx.append(mx_tiles("g_%d" % qt, Q_TILE))
+            quantize(g_mx[qt], 0, Q_TILE, g_bf[:])
+
+        y_banks = []
+        for qt in range(Q_TILES):
+            y_banks.append(psum.tile([P, V], F32, name="y_bank%d" % qt))
+            multiply(y_banks[qt][:], mx_columns(g_mx[qt], 0, Q_TILE), mx_columns(z_mx, 0, V), True, True)
+        neg_max, exps, totals = [], [], []
+        for qt in range(Q_TILES):
+            neg_max.append(sbuf("neg_max%d" % qt, [P, 1], F32))
+            nc.vector.tensor_reduce(out=neg_max[qt][:], in_=y_banks[qt][:], axis=mybir.AxisListType.X, op=ALU.max, negate=True)
+        for qt in range(Q_TILES):
+            exps.append(sbuf("exp%d" % qt, [P, V], F32))
+            totals.append(sbuf("total%d" % qt, [P, 1], F32))
+            nc.scalar.activation(out=exps[qt][:], in_=y_banks[qt][:], func=ACT.Exp, bias=neg_max[qt][:], accum_out=totals[qt][:])
+
+        def inverse_total(qt):
+            inverse = sbuf("inverse%d" % qt, [P, 1], F32)
+            nc.vector.reciprocal(out=inverse[:], in_=totals[qt][:])
+            return inverse
+
+        def normalise_on_vector(qt, width, inverse):
+            prob = sbuf("prob%d" % qt, [P, width], F32)
+            nc.vector.tensor_scalar(out=prob[:], in0=exps[qt][:, :width], scalar1=inverse[:], scalar2=None, op0=ALU.mult)
+            nc.sync.dma_start(out=out[qt * Q_TILE : (qt + 1) * Q_TILE, :width], in_=prob[:])
+
+        normalise_on_vector(0, V, inverse_total(0))
+        last_inverse = inverse_total(1)
+        normalise_on_vector(1, V_HALF, last_inverse)
+        prob_hi = sbuf("prob_hi", [P, V_HALF], F32)
+        nc.scalar.activation(out=prob_hi[:], in_=exps[1][:, V_HALF:], func=ACT.Copy, scale=last_inverse[:])
+        nc.scalar.dma_start(out=out[Q_TILE:, V_HALF:], in_=prob_hi[:])

@@ -24,10 +24,12 @@ RUN = 4
 QUADRANT = 32
 SCALE_ROWS = 4
 V_HALF = V // 2
+SLAB_ORDER = (2, 3, 0, 1)
 V_CHUNK = 128
 CHUNKS = V // V_CHUNK
 Q_TILE = 128
 Q_TILES = J // Q_TILE
+X_HEAD = T // 8
 
 
 def tile_picked_zproto_none_p_kernel(tc, x_words, x_scales, w1, w2, eT, offs, out):
@@ -68,8 +70,8 @@ def tile_picked_zproto_none_p_kernel(tc, x_words, x_scales, w1, w2, eT, offs, ou
             )
             return grouped
 
-        def cast_queries(grouped, rows, c0, c1):
-            on_scalar(
+        def cast_queries(grouped, rows, c0, c1, copy):
+            copy(
                 out=grouped[:, c0 * PACK : c1 * PACK].rearrange("p (c a j) -> p c j a", a=RUN, j=PACK),
                 in_=rows[:, :, c0:c1].rearrange("p j (c a) -> p c j a", a=RUN),
             )
@@ -93,102 +95,108 @@ def tile_picked_zproto_none_p_kernel(tc, x_words, x_scales, w1, w2, eT, offs, ou
         def class_passes(bank, c, o, w1_mx, words):
             v0 = c * V_CHUNK
             v_in = v0 % V_HALF
-            for t in range(SLABS):
+            for n, t in enumerate(SLAB_ORDER):
                 for d in range(D):
                     moving = (
                         words[:, d, v_in : v_in + V_CHUNK].bitcast(FP8X4),
                         member_scales[SCALE_ROWS * o : P, d, v0 : v0 + V_CHUNK],
                     )
-                    first = o == 0 and t == 0 and d == 0
-                    last = o == PASSES - 1 and t == SLABS - 1 and d == D - 1
+                    first = o == 0 and n == 0 and d == 0
+                    last = o == PASSES - 1 and n == SLABS - 1 and d == D - 1
                     multiply(bank[:, t, :], mx_columns(w1_mx, t * P, (t + 1) * P), moving, first, last)
 
         def query_passes(bank, qt, o, w2_mx, e_mx):
-            for t in range(SLABS):
-                first = o == 0 and t == 0
-                last = o == PASSES - 1 and t == SLABS - 1
+            for n, t in enumerate(SLAB_ORDER):
+                first = o == 0 and n == 0
+                last = o == PASSES - 1 and n == SLABS - 1
                 multiply(bank[:, t, :], mx_columns(w2_mx, t * P, (t + 1) * P), mx_columns(e_mx, qt * Q_TILE, (qt + 1) * Q_TILE), first, last)
 
         offsets = sbuf("offsets", [P, S // 16], U16)
         scale_store = sbuf("scale_store", [P, T], U8)
         member_scales = sbuf("member_scales", [P, D, V], U8)
+        half_slabs, half_h = SLABS // 2, H // 2
 
-        w1_rows0 = load_pass(sbuf("w1_raw0", [P, PACK * H], F32)[:], w1, 0)
-        nc.sync.dma_start(offsets[:], offs)
-        nc.vector.memset(scale_store[:].bitcast(I32), 0)
-        nc.sync.dma_start(out=scale_store[0:P:4, :].bitcast(I32), in_=x_scales.rearrange("o m c -> m o c").bitcast(I32))
-        w1_rows1 = load_pass(sbuf("w1_raw1", [P, PACK * H], F32)[:], w1, 1)
-        x_store0 = load_words(0)
+        def words_of(o):
+            return x_words[o].rearrange("p n r -> p (n r)").bitcast(I32)
 
-        picked_scales = sbuf("picked_scales", [P, S], U8)
-        nc.vector.tensor_copy(out=picked_scales[:], in_=scale_store[:].indirect(offsets[:]))
-        nc.vector.tensor_copy(out=member_scales[:], in_=picked_scales[:].rearrange("p (v d) -> p d v", d=D))
-        scale_rows = member_scales[:].rearrange("p d v -> p (d v)").bitcast(I32)
-        for o in range(PASSES):
+        def move_scale_rows(o):
             for r in range(1, SCALE_ROWS):
                 nc.sync.dma_start(
                     out=scale_rows[SCALE_ROWS * o + r : P : QUADRANT, :], in_=scale_rows[SCALE_ROWS * o + 8 * r : P : QUADRANT, :]
                 )
 
+        def weight_pass(name, rows, reuse_hi=None, reuse_lo=None):
+            hi = cast_slabs(name + "_bf_hi", rows, half_slabs, SLABS, on_vector, reuse_hi)
+            lo = cast_slabs(name + "_bf_lo", rows, 0, half_slabs, on_scalar, reuse_lo)
+            mx = mx_tiles(name, H)
+            quantize(mx, half_h, H, hi[:])
+            quantize(mx, 0, half_h, lo[:])
+            return mx
+
+        x_store0 = sbuf("x_store0", [P, T], I32)
+        nc.sync.dma_start(out=x_store0[:, :X_HEAD], in_=words_of(0)[:, :X_HEAD])
+        nc.sync.dma_start(offsets[:], offs)
+        nc.gpsimd.memset(scale_store[:, : T // 2].bitcast(I32), 0)
+        nc.vector.memset(scale_store[:, T // 2 :].bitcast(I32), 0)
+        nc.sync.dma_start(out=scale_store[0:P:4, :].bitcast(I32), in_=x_scales.rearrange("o m c -> m o c").bitcast(I32))
+        nc.sync.dma_start(out=x_store0[:, X_HEAD:], in_=words_of(0)[:, X_HEAD:])
+        w1_rows0 = load_pass(sbuf("w1_raw0", [P, PACK * H], F32)[:], w1, 0)
+
+        picked_scales = sbuf("picked_scales", [P, S], U8)
+        nc.vector.tensor_copy(out=picked_scales[:], in_=scale_store[:].indirect(offsets[:]))
+        nc.vector.tensor_copy(out=member_scales[:], in_=picked_scales[:].rearrange("p (v d) -> p d v", d=D))
+        scale_rows = member_scales[:].rearrange("p d v -> p (d v)").bitcast(I32)
+        move_scale_rows(0)
+        move_scale_rows(1)
         x_store1 = load_words(1, reuse="picked_scales")
+
+        picked0 = [gather_words(x_store0, 0, half) for half in range(2)]
+        mid_raw = sbuf("mid_raw", [P, PACK * 2 * H], F32, reuse="x_store0")
+        w1_rows1 = load_pass(mid_raw[:, : PACK * H], w1, 1)
+        w2_rows0 = load_pass(mid_raw[:, PACK * H :], w2, 0)
         w1_bf0 = cast_slabs("w1_bf0", w1_rows0, 0, SLABS, on_scalar)
         w1_mx0 = mx_tiles("w1_0", H)
         quantize(w1_mx0, 0, H, w1_bf0[:])
-        e_rows0 = load_pass(sbuf("e_raw0", [P, PACK * J], F32, reuse="w1_bf0")[:], eT, 0)
-        w1_bf1 = cast_slabs("w1_bf1", w1_rows1, 0, SLABS, on_scalar)
-        w1_mx1 = mx_tiles("w1_1", H)
-        quantize(w1_mx1, 0, H, w1_bf1[:])
-        w2_rows0 = load_pass(sbuf("w2_raw0", [P, PACK * H], F32, reuse="w1_bf1")[:], w2, 0)
-        picked0 = [gather_words(x_store0, 0, half) for half in range(2)]
-        last_raw = sbuf("last_raw", [P, PACK * (H + J)], F32, reuse="x_store0")
-        w2_rows1 = load_pass(last_raw[:, : PACK * H], w2, 1)
-        e_rows1 = load_pass(last_raw[:, PACK * H :], eT, 1)
+        last_raw = sbuf("last_raw", [P, PACK * (H + 2 * J)], F32, reuse="w1_raw0")
+        e_rows0 = load_pass(last_raw[:, : PACK * J], eT, 0)
+        w2_rows1 = load_pass(last_raw[:, PACK * J : PACK * (H + J)], w2, 1)
+        e_rows1 = load_pass(last_raw[:, PACK * (H + J) :], eT, 1)
 
         z_banks = []
         for c in range(CHUNKS):
             z_banks.append(psum.tile([P, SLABS, V_CHUNK], F32, name="z_bank%d" % c))
             class_passes(z_banks[c], c, 0, w1_mx0, picked0[c * V_CHUNK // V_HALF])
         picked1 = [gather_words(x_store1, 1, half) for half in range(2)]
+        w1_mx1 = weight_pass("w1_1", w1_rows1)
         for c in range(CHUNKS):
             class_passes(z_banks[c], c, 1, w1_mx1, picked1[c * V_CHUNK // V_HALF])
+        w2_mx0 = weight_pass("w2_0", w2_rows0)
+
+        z_bf = sbuf("z_bf", [P, V * PACK], BF16, reuse="x_store0")
+        for c in range(CHUNKS):
+            z_out = z_bf[:, c * V_CHUNK * PACK : (c + 1) * V_CHUNK * PACK].rearrange("p (v t) -> p v t", t=SLABS)
+            z_in = z_banks[c][:].rearrange("p t v -> p v t")
+            if c in (2,):
+                nc.vector.tensor_scalar(out=z_out, in0=z_in, scalar1=1.0 / D, scalar2=None, op0=ALU.mult)
+            else:
+                nc.scalar.activation(out=z_out, in_=z_in, func=ACT.Copy, scale=1.0 / D)
 
         e_bf0 = sbuf("e_bf0", [P, J * PACK], BF16)
-        cast_queries(e_bf0, e_rows0, 0, J)
-        z_bf = sbuf("z_bf", [P, V * PACK], BF16, reuse="w1_bf0")
-        for c in range(CHUNKS):
-            nc.scalar.activation(
-                out=z_bf[:, c * V_CHUNK * PACK : (c + 1) * V_CHUNK * PACK].rearrange("p (v t) -> p v t", t=SLABS),
-                in_=z_banks[c][:].rearrange("p t v -> p v t"),
-                func=ACT.Copy,
-                scale=1.0 / D,
-            )
-
-        half_slabs, half_h = SLABS // 2, H // 2
-        w2_bf0_lo = cast_slabs("w2_bf0_lo", w2_rows0, 0, half_slabs, on_vector, reuse="picked_scales")
-        w2_bf0_hi = cast_slabs("w2_bf0_hi", w2_rows0, half_slabs, SLABS, on_vector)
-        w2_mx0 = mx_tiles("w2_0", H)
-        quantize(w2_mx0, 0, half_h, w2_bf0_lo[:])
-        quantize(w2_mx0, half_h, H, w2_bf0_hi[:])
-        e_mx0 = mx_tiles("e_0", J, reuse="picked_scales")
+        cast_queries(e_bf0, e_rows0, 0, J, on_vector)
+        e_mx0 = mx_tiles("e_0", J)
         quantize(e_mx0, 0, J, e_bf0[:])
         g_banks = []
         for qt in range(Q_TILES):
             g_banks.append(psum.tile([P, SLABS, Q_TILE], F32, name="g_bank%d" % qt))
             query_passes(g_banks[qt], qt, 0, w2_mx0, e_mx0)
 
-        w2_bf1_lo = cast_slabs("w2_bf1_lo", w2_rows1, 0, half_slabs, on_vector, reuse="w2_bf0_hi")
-        w2_bf1_hi = cast_slabs("w2_bf1_hi", w2_rows1, half_slabs, SLABS, on_scalar, reuse="picked1_1")
-        w2_mx1 = mx_tiles("w2_1", H)
-        quantize(w2_mx1, 0, half_h, w2_bf1_lo[:])
-        quantize(w2_mx1, half_h, H, w2_bf1_hi[:])
-        e_bf1 = sbuf("e_bf1", [P, J * PACK], BF16, reuse="picked1_0")
-        cast_queries(e_bf1, e_rows1, 0, Q_TILE)
+        w2_mx1 = weight_pass("w2_1", w2_rows1, reuse_lo="picked1_1")
         e_mx1 = mx_tiles("e_1", J)
-        quantize(e_mx1, 0, Q_TILE, e_bf1[:, : Q_TILE * PACK])
-        query_passes(g_banks[0], 0, 1, w2_mx1, e_mx1)
-        cast_queries(e_bf1, e_rows1, Q_TILE, J)
-        quantize(e_mx1, Q_TILE, J, e_bf1[:, Q_TILE * PACK :])
-        query_passes(g_banks[1], 1, 1, w2_mx1, e_mx1)
+        for qt, copy, reuse in ((0, on_vector, None), (1, on_scalar, "picked1_0")):
+            e_bf1 = sbuf("e_bf1_%d" % qt, [P, Q_TILE * PACK], BF16, reuse)
+            cast_queries(e_bf1, e_rows1[:, :, qt * Q_TILE : (qt + 1) * Q_TILE], 0, Q_TILE, copy)
+            quantize(e_mx1, qt * Q_TILE, (qt + 1) * Q_TILE, e_bf1[:])
+            query_passes(g_banks[qt], qt, 1, w2_mx1, e_mx1)
 
         z_mx = mx_tiles("z", V, reuse="picked1_0")
         quantize(z_mx, 0, V, z_bf[:])

@@ -24,12 +24,10 @@ RUN = 4
 QUADRANT = 32
 SCALE_ROWS = 4
 V_HALF = V // 2
-SLAB_ORDER = (2, 3, 0, 1)
 V_CHUNK = 128
 CHUNKS = V // V_CHUNK
 Q_TILE = 128
 Q_TILES = J // Q_TILE
-X_HEAD = T // 8
 
 
 def tile_picked_zproto_none_p_kernel(tc, x_words, x_scales, w1, w2, eT, offs, out):
@@ -92,21 +90,21 @@ def tile_picked_zproto_none_p_kernel(tc, x_words, x_scales, w1, w2, eT, offs, ou
                 out=dst, lhsT=stationary[0], lhsT_scale=stationary[1], rhs=moving[0], rhs_scale=moving[1], start=start, stop=stop
             )
 
-        def class_passes(bank, c, o, w1_mx, words):
+        def class_passes(bank, c, o, w1_mx, words, slabs):
             v0 = c * V_CHUNK
             v_in = v0 % V_HALF
-            for n, t in enumerate(SLAB_ORDER):
+            for t in slabs:
                 for d in range(D):
                     moving = (
                         words[:, d, v_in : v_in + V_CHUNK].bitcast(FP8X4),
                         member_scales[SCALE_ROWS * o : P, d, v0 : v0 + V_CHUNK],
                     )
-                    first = o == 0 and n == 0 and d == 0
-                    last = o == PASSES - 1 and n == SLABS - 1 and d == D - 1
+                    first = o == 0 and t == 0 and d == 0
+                    last = o == PASSES - 1 and t == SLABS - 1 and d == D - 1
                     multiply(bank[:, t, :], mx_columns(w1_mx, t * P, (t + 1) * P), moving, first, last)
 
         def query_passes(bank, qt, o, w2_mx, e_mx):
-            for n, t in enumerate(SLAB_ORDER):
+            for n, t in enumerate((2, 3, 0, 1)):
                 first = o == 0 and n == 0
                 last = o == PASSES - 1 and n == SLABS - 1
                 multiply(bank[:, t, :], mx_columns(w2_mx, t * P, (t + 1) * P), mx_columns(e_mx, qt * Q_TILE, (qt + 1) * Q_TILE), first, last)
@@ -115,9 +113,6 @@ def tile_picked_zproto_none_p_kernel(tc, x_words, x_scales, w1, w2, eT, offs, ou
         scale_store = sbuf("scale_store", [P, T], U8)
         member_scales = sbuf("member_scales", [P, D, V], U8)
         half_slabs, half_h = SLABS // 2, H // 2
-
-        def words_of(o):
-            return x_words[o].rearrange("p n r -> p (n r)").bitcast(I32)
 
         def move_scale_rows(o):
             for r in range(1, SCALE_ROWS):
@@ -133,14 +128,12 @@ def tile_picked_zproto_none_p_kernel(tc, x_words, x_scales, w1, w2, eT, offs, ou
             quantize(mx, 0, half_h, lo[:])
             return mx
 
-        x_store0 = sbuf("x_store0", [P, T], I32)
-        nc.sync.dma_start(out=x_store0[:, :X_HEAD], in_=words_of(0)[:, :X_HEAD])
-        nc.sync.dma_start(offsets[:], offs)
-        nc.gpsimd.memset(scale_store[:, : T // 2].bitcast(I32), 0)
-        nc.vector.memset(scale_store[:, T // 2 :].bitcast(I32), 0)
-        nc.sync.dma_start(out=scale_store[0:P:4, :].bitcast(I32), in_=x_scales.rearrange("o m c -> m o c").bitcast(I32))
-        nc.sync.dma_start(out=x_store0[:, X_HEAD:], in_=words_of(0)[:, X_HEAD:])
         w1_rows0 = load_pass(sbuf("w1_raw0", [P, PACK * H], F32)[:], w1, 0)
+        nc.sync.dma_start(offsets[:], offs)
+        nc.vector.memset(scale_store[:].bitcast(I32), 0)
+        nc.sync.dma_start(out=scale_store[0:P:4, :].bitcast(I32), in_=x_scales.rearrange("o m c -> m o c").bitcast(I32))
+        x_store0 = load_words(0)
+        x_store1 = load_words(1)
 
         picked_scales = sbuf("picked_scales", [P, S], U8)
         nc.vector.tensor_copy(out=picked_scales[:], in_=scale_store[:].indirect(offsets[:]))
@@ -148,49 +141,62 @@ def tile_picked_zproto_none_p_kernel(tc, x_words, x_scales, w1, w2, eT, offs, ou
         scale_rows = member_scales[:].rearrange("p d v -> p (d v)").bitcast(I32)
         move_scale_rows(0)
         move_scale_rows(1)
-        x_store1 = load_words(1, reuse="picked_scales")
 
         picked0 = [gather_words(x_store0, 0, half) for half in range(2)]
-        mid_raw = sbuf("mid_raw", [P, PACK * 2 * H], F32, reuse="x_store0")
+        mid_raw = sbuf("mid_raw", [P, PACK * (H + J)], F32, reuse="picked_scales")
         w1_rows1 = load_pass(mid_raw[:, : PACK * H], w1, 1)
-        w2_rows0 = load_pass(mid_raw[:, PACK * H :], w2, 0)
+        e_rows0 = load_pass(mid_raw[:, PACK * H :], eT, 0)
         w1_bf0 = cast_slabs("w1_bf0", w1_rows0, 0, SLABS, on_scalar)
         w1_mx0 = mx_tiles("w1_0", H)
         quantize(w1_mx0, 0, H, w1_bf0[:])
-        last_raw = sbuf("last_raw", [P, PACK * (H + 2 * J)], F32, reuse="w1_raw0")
-        e_rows0 = load_pass(last_raw[:, : PACK * J], eT, 0)
-        w2_rows1 = load_pass(last_raw[:, PACK * J : PACK * (H + J)], w2, 1)
-        e_rows1 = load_pass(last_raw[:, PACK * (H + J) :], eT, 1)
+        last_raw = sbuf("last_raw", [P, PACK * (2 * H + J)], F32, reuse="x_store0")
+        w2_rows0 = load_pass(last_raw[:, : PACK * H], w2, 0)
+        w2_rows1 = load_pass(last_raw[:, PACK * H : PACK * 2 * H], w2, 1)
+        e_rows1 = load_pass(last_raw[:, PACK * 2 * H :], eT, 1)
 
-        z_banks = []
-        for c in range(CHUNKS):
-            z_banks.append(psum.tile([P, SLABS, V_CHUNK], F32, name="z_bank%d" % c))
-            class_passes(z_banks[c], c, 0, w1_mx0, picked0[c * V_CHUNK // V_HALF])
-        picked1 = [gather_words(x_store1, 1, half) for half in range(2)]
-        w1_mx1 = weight_pass("w1_1", w1_rows1)
-        for c in range(CHUNKS):
-            class_passes(z_banks[c], c, 1, w1_mx1, picked1[c * V_CHUNK // V_HALF])
-        w2_mx0 = weight_pass("w2_0", w2_rows0)
-
-        z_bf = sbuf("z_bf", [P, V * PACK], BF16, reuse="x_store0")
-        for c in range(CHUNKS):
-            z_out = z_bf[:, c * V_CHUNK * PACK : (c + 1) * V_CHUNK * PACK].rearrange("p (v t) -> p v t", t=SLABS)
-            z_in = z_banks[c][:].rearrange("p t v -> p v t")
-            if c in (2,):
+        def halve(bank, dst, on_vector_engine):
+            z_out = dst.rearrange("p (v t) -> p v t", t=SLABS)
+            z_in = bank[:].rearrange("p t v -> p v t")
+            if on_vector_engine:
                 nc.vector.tensor_scalar(out=z_out, in0=z_in, scalar1=1.0 / D, scalar2=None, op0=ALU.mult)
             else:
                 nc.scalar.activation(out=z_out, in_=z_in, func=ACT.Copy, scale=1.0 / D)
 
+        lower, upper = range(half_slabs), range(half_slabs, SLABS)
+        z_banks = []
+        for c in range(CHUNKS):
+            z_banks.append(psum.tile([P, SLABS, V_CHUNK], F32, name="z_bank%d" % c, tag="z_bank%d" % c))
+            class_passes(z_banks[c], c, 0, w1_mx0, picked0[c * V_CHUNK // V_HALF], range(SLABS))
+        picked1 = [gather_words(x_store1, 1, half) for half in range(2)]
+        w1_bf1_lo = cast_slabs("w1_bf1_lo", w1_rows1, 0, half_slabs, on_scalar)
+        w1_bf1_hi = cast_slabs("w1_bf1_hi", w1_rows1, half_slabs, SLABS, on_scalar)
+        w1_mx1 = mx_tiles("w1_1", H)
+        quantize(w1_mx1, 0, half_h, w1_bf1_lo[:])
+        quantize(w1_mx1, half_h, H, w1_bf1_hi[:])
+        for c in range(CHUNKS):
+            class_passes(z_banks[c], c, 1, w1_mx1, picked1[c * V_CHUNK // V_HALF], range(SLABS))
+
+        w2_bf0_lo = cast_slabs("w2_bf0_lo", w2_rows0, 0, half_slabs, on_vector, reuse="w1_bf1_hi")
+        w2_bf0_hi = cast_slabs("w2_bf0_hi", w2_rows0, half_slabs, SLABS, on_vector)
+        w2_mx0 = mx_tiles("w2_0", H)
+        quantize(w2_mx0, 0, half_h, w2_bf0_lo[:])
+        quantize(w2_mx0, half_h, H, w2_bf0_hi[:])
         e_bf0 = sbuf("e_bf0", [P, J * PACK], BF16)
-        cast_queries(e_bf0, e_rows0, 0, J, on_vector)
-        e_mx0 = mx_tiles("e_0", J)
+        cast_queries(e_bf0, e_rows0, 0, J, on_scalar)
+        e_mx0 = mx_tiles("e_0", J, reuse="w1_bf1_hi")
         quantize(e_mx0, 0, J, e_bf0[:])
+
+        z_width = V_CHUNK * PACK
+        z_bf = sbuf("z_bf", [P, (CHUNKS - 1) * z_width], BF16, reuse="picked_scales")
+        for c in range(CHUNKS - 1):
+            halve(z_banks[c], z_bf[:, c * z_width : (c + 1) * z_width], False)
+
         g_banks = []
         for qt in range(Q_TILES):
-            g_banks.append(psum.tile([P, SLABS, Q_TILE], F32, name="g_bank%d" % qt))
+            g_banks.append(psum.tile([P, SLABS, Q_TILE], F32, name="g_bank%d" % qt, tag="z_bank%d" % (qt + 1)))
             query_passes(g_banks[qt], qt, 0, w2_mx0, e_mx0)
 
-        w2_mx1 = weight_pass("w2_1", w2_rows1, reuse_lo="picked1_1")
+        w2_mx1 = weight_pass("w2_1", w2_rows1)
         e_mx1 = mx_tiles("e_1", J)
         for qt, copy, reuse in ((0, on_vector, None), (1, on_scalar, "picked1_0")):
             e_bf1 = sbuf("e_bf1_%d" % qt, [P, Q_TILE * PACK], BF16, reuse)
@@ -198,8 +204,12 @@ def tile_picked_zproto_none_p_kernel(tc, x_words, x_scales, w1, w2, eT, offs, ou
             quantize(e_mx1, qt * Q_TILE, (qt + 1) * Q_TILE, e_bf1[:])
             query_passes(g_banks[qt], qt, 1, w2_mx1, e_mx1)
 
+        z_bf3 = sbuf("z_bf3", [P, z_width], BF16, reuse="x_store0")
+        halve(z_banks[3], z_bf3[:], False)
         z_mx = mx_tiles("z", V, reuse="picked1_0")
-        quantize(z_mx, 0, V, z_bf[:])
+        quantize(z_mx, 0, V_HALF, z_bf[:, : 2 * z_width])
+        quantize(z_mx, V_HALF, V - V_CHUNK, z_bf[:, 2 * z_width :])
+        quantize(z_mx, V - V_CHUNK, V, z_bf3[:])
         g_mx = []
         for qt in range(Q_TILES):
             g_bf = sbuf("g_bf%d" % qt, [P, Q_TILE * PACK], BF16)

@@ -169,21 +169,23 @@ def tile_picked_zproto_none_p_kernel(tc, x_words, x_scales, w1, w2, eT, offs, ou
             class_passes(z_banks[c], c, 0, w1_mx0, picked0[c * V_CHUNK // V_HALF], range(SLABS))
         picked1 = [gather_words(x_store1, 1, half) for half in range(2)]
         w1_bf1_lo = cast_slabs("w1_bf1_lo", w1_rows1, 0, half_slabs, on_scalar)
-        w1_bf1_hi = cast_slabs("w1_bf1_hi", w1_rows1, half_slabs, SLABS, on_scalar)
+        w1_bf1_third = cast_slabs("w1_bf1_third", w1_rows1, half_slabs, SLABS - 1, on_scalar)
         w1_mx1 = mx_tiles("w1_1", H)
         quantize(w1_mx1, 0, half_h, w1_bf1_lo[:])
-        quantize(w1_mx1, half_h, H, w1_bf1_hi[:])
+        w1_bf1_last = cast_slabs("w1_bf1_last", w1_rows1, SLABS - 1, SLABS, on_vector, reuse="w1_bf1_lo")
+        quantize(w1_mx1, half_h, H - P, w1_bf1_third[:])
+        quantize(w1_mx1, H - P, H, w1_bf1_last[:])
         for c in range(CHUNKS):
             class_passes(z_banks[c], c, 1, w1_mx1, picked1[c * V_CHUNK // V_HALF], range(SLABS))
 
-        w2_bf0_lo = cast_slabs("w2_bf0_lo", w2_rows0, 0, half_slabs, on_vector, reuse="w1_bf1_hi")
+        w2_bf0_lo = cast_slabs("w2_bf0_lo", w2_rows0, 0, half_slabs, on_vector, reuse="w1_bf1_lo")
         w2_bf0_hi = cast_slabs("w2_bf0_hi", w2_rows0, half_slabs, SLABS, on_vector)
         w2_mx0 = mx_tiles("w2_0", H)
         quantize(w2_mx0, 0, half_h, w2_bf0_lo[:])
         quantize(w2_mx0, half_h, H, w2_bf0_hi[:])
         e_bf0 = sbuf("e_bf0", [P, J * PACK], BF16)
         cast_queries(e_bf0, e_rows0, 0, J, on_scalar)
-        e_mx0 = mx_tiles("e_0", J, reuse="w1_bf1_hi")
+        e_mx0 = mx_tiles("e_0", J, reuse="w1_bf1_lo")
         quantize(e_mx0, 0, J, e_bf0[:])
 
         z_width = V_CHUNK * PACK

@@ -90,29 +90,11 @@ def tile_picked_zproto_none_p_kernel(tc, x_words, x_scales, w1, w2, eT, offs, ou
                 out=dst, lhsT=stationary[0], lhsT_scale=stationary[1], rhs=moving[0], rhs_scale=moving[1], start=start, stop=stop
             )
 
-        def class_passes(bank, c, o, w1_mx, words, slabs):
-            v0 = c * V_CHUNK
-            v_in = v0 % V_HALF
-            for t in slabs:
-                for d in range(D):
-                    moving = (
-                        words[:, d, v_in : v_in + V_CHUNK].bitcast(FP8X4),
-                        member_scales[SCALE_ROWS * o : P, d, v0 : v0 + V_CHUNK],
-                    )
-                    first = o == 0 and t == 0 and d == 0
-                    last = o == PASSES - 1 and t == SLABS - 1 and d == D - 1
-                    multiply(bank[:, t, :], mx_columns(w1_mx, t * P, (t + 1) * P), moving, first, last)
-
-        def query_passes(bank, qt, o, w2_mx, e_mx):
-            for n, t in enumerate((2, 3, 0, 1)):
-                first = o == 0 and n == 0
-                last = o == PASSES - 1 and n == SLABS - 1
-                multiply(bank[:, t, :], mx_columns(w2_mx, t * P, (t + 1) * P), mx_columns(e_mx, qt * Q_TILE, (qt + 1) * Q_TILE), first, last)
-
         offsets = sbuf("offsets", [P, S // 16], U16)
         scale_store = sbuf("scale_store", [P, T], U8)
         member_scales = sbuf("member_scales", [P, D, V], U8)
-        half_slabs, half_h = SLABS // 2, H // 2
+        half_slabs, half_h, half_q = SLABS // 2, H // 2, Q_TILE // 2
+        lower, upper = range(half_slabs), range(half_slabs, SLABS)
 
         def move_scale_rows(o):
             for r in range(1, SCALE_ROWS):
@@ -120,13 +102,29 @@ def tile_picked_zproto_none_p_kernel(tc, x_words, x_scales, w1, w2, eT, offs, ou
                     out=scale_rows[SCALE_ROWS * o + r : P : QUADRANT, :], in_=scale_rows[SCALE_ROWS * o + 8 * r : P : QUADRANT, :]
                 )
 
-        def weight_pass(name, rows, reuse_hi=None, reuse_lo=None):
-            hi = cast_slabs(name + "_bf_hi", rows, half_slabs, SLABS, on_vector, reuse_hi)
-            lo = cast_slabs(name + "_bf_lo", rows, 0, half_slabs, on_scalar, reuse_lo)
-            mx = mx_tiles(name, H)
-            quantize(mx, half_h, H, hi[:])
-            quantize(mx, 0, half_h, lo[:])
-            return mx
+        def halve(bank, dst):
+            nc.scalar.activation(
+                out=dst.rearrange("p (v t) -> p v t", t=SLABS), in_=bank[:].rearrange("p t v -> p v t"), func=ACT.Copy, scale=1.0 / D
+            )
+
+        def tile_passes(bank, o, w2_mx, e_mx, slabs):
+            for n, t in enumerate(slabs):
+                first = o == 0 and n == 0
+                last = o == PASSES - 1 and n == SLABS - 1
+                multiply(bank[:, t, :], mx_columns(w2_mx, t * P, (t + 1) * P), mx_columns(e_mx, 0, Q_TILE), first, last)
+
+        def chunk_passes(bank, c, o, w1_mx, words, slabs):
+            v0 = c * V_CHUNK
+            v_in = v0 % V_HALF
+            for n, t in enumerate(slabs):
+                for d in range(D):
+                    moving = (
+                        words[:, d, v_in : v_in + V_CHUNK].bitcast(FP8X4),
+                        member_scales[SCALE_ROWS * o : P, d, v0 : v0 + V_CHUNK],
+                    )
+                    first = o == 0 and n == 0 and d == 0
+                    last = o == PASSES - 1 and n == SLABS - 1 and d == D - 1
+                    multiply(bank[:, t, :], mx_columns(w1_mx, t * P, (t + 1) * P), moving, first, last)
 
         w1_rows0 = load_pass(sbuf("w1_raw0", [P, PACK * H], F32)[:], w1, 0)
         nc.sync.dma_start(offsets[:], offs)
@@ -143,73 +141,89 @@ def tile_picked_zproto_none_p_kernel(tc, x_words, x_scales, w1, w2, eT, offs, ou
         move_scale_rows(1)
 
         picked0 = [gather_words(x_store0, 0, half) for half in range(2)]
-        mid_raw = sbuf("mid_raw", [P, PACK * (H + J)], F32, reuse="picked_scales")
-        w1_rows1 = load_pass(mid_raw[:, : PACK * H], w1, 1)
-        e_rows0 = load_pass(mid_raw[:, PACK * H :], eT, 0)
+        w_width, e_width = PACK * H, PACK * Q_TILE
+        mid_raw = sbuf("mid_raw", [P, w_width + e_width], F32, reuse="picked_scales")
+        w1_rows1 = load_pass(mid_raw[:, :w_width], w1, 1)
+        e_rows = {}
+        e_rows[0, 0] = load_pass(mid_raw[:, w_width:], eT[:, :Q_TILE], 0)
         w1_bf0 = cast_slabs("w1_bf0", w1_rows0, 0, SLABS, on_scalar)
         w1_mx0 = mx_tiles("w1_0", H)
         quantize(w1_mx0, 0, H, w1_bf0[:])
-        last_raw = sbuf("last_raw", [P, PACK * (2 * H + J)], F32, reuse="x_store0")
-        w2_rows0 = load_pass(last_raw[:, : PACK * H], w2, 0)
-        w2_rows1 = load_pass(last_raw[:, PACK * H : PACK * 2 * H], w2, 1)
-        e_rows1 = load_pass(last_raw[:, PACK * 2 * H :], eT, 1)
+        last_raw = sbuf("last_raw", [P, 2 * w_width + 3 * e_width], F32, reuse="x_store0")
+        w2_rows0 = load_pass(last_raw[:, :w_width], w2, 0)
+        w2_rows1 = load_pass(last_raw[:, w_width : 2 * w_width], w2, 1)
+        for n, (o, qt) in enumerate(((1, 0), (0, 1), (1, 1))):
+            c0 = 2 * w_width + n * e_width
+            e_rows[o, qt] = load_pass(last_raw[:, c0 : c0 + e_width], eT[:, qt * Q_TILE : (qt + 1) * Q_TILE], o)
 
-        def halve(bank, dst, on_vector_engine):
-            z_out = dst.rearrange("p (v t) -> p v t", t=SLABS)
-            z_in = bank[:].rearrange("p t v -> p v t")
-            if on_vector_engine:
-                nc.vector.tensor_scalar(out=z_out, in0=z_in, scalar1=1.0 / D, scalar2=None, op0=ALU.mult)
-            else:
-                nc.scalar.activation(out=z_out, in_=z_in, func=ACT.Copy, scale=1.0 / D)
-
-        lower, upper = range(half_slabs), range(half_slabs, SLABS)
         z_banks = []
-        for c in range(CHUNKS):
+        for c in range(CHUNKS - 1):
             z_banks.append(psum.tile([P, SLABS, V_CHUNK], F32, name="z_bank%d" % c, tag="z_bank%d" % c))
-            class_passes(z_banks[c], c, 0, w1_mx0, picked0[c * V_CHUNK // V_HALF], range(SLABS))
+            chunk_passes(z_banks[c], c, 0, w1_mx0, picked0[c * V_CHUNK // V_HALF], range(SLABS))
         picked1 = [gather_words(x_store1, 1, half) for half in range(2)]
         w1_bf1_lo = cast_slabs("w1_bf1_lo", w1_rows1, 0, half_slabs, on_scalar)
-        w1_bf1_third = cast_slabs("w1_bf1_third", w1_rows1, half_slabs, SLABS - 1, on_scalar)
+        w1_bf1_hi = cast_slabs("w1_bf1_hi", w1_rows1, half_slabs, SLABS, on_vector)
         w1_mx1 = mx_tiles("w1_1", H)
+        quantize(w1_mx1, half_h, H, w1_bf1_hi[:])
         quantize(w1_mx1, 0, half_h, w1_bf1_lo[:])
-        w1_bf1_last = cast_slabs("w1_bf1_last", w1_rows1, SLABS - 1, SLABS, on_vector, reuse="w1_bf1_lo")
-        quantize(w1_mx1, half_h, H - P, w1_bf1_third[:])
-        quantize(w1_mx1, H - P, H, w1_bf1_last[:])
-        for c in range(CHUNKS):
-            class_passes(z_banks[c], c, 1, w1_mx1, picked1[c * V_CHUNK // V_HALF], range(SLABS))
+        hi_first = tuple(upper) + tuple(lower)
+        for c in range(CHUNKS - 1):
+            chunk_passes(z_banks[c], c, 1, w1_mx1, picked1[c * V_CHUNK // V_HALF], hi_first)
 
-        w2_bf0_lo = cast_slabs("w2_bf0_lo", w2_rows0, 0, half_slabs, on_vector, reuse="w1_bf1_lo")
+        e_mx = {}
+
+        def cast_tile(o, qt, copy):
+            grouped = sbuf("e_bf%d_%d" % (o, qt), [P, e_width], BF16)
+            cast_queries(grouped, e_rows[o, qt], 0, Q_TILE, copy)
+            e_mx[o, qt] = mx_tiles("e_%d_%d" % (o, qt), Q_TILE)
+            return grouped
+
+        e_bf00 = cast_tile(0, 0, on_scalar)
+        quantize(e_mx[0, 0], 0, Q_TILE, e_bf00[:])
+
+        z_width = V_CHUNK * PACK
+        z_bf = sbuf("z_bf", [P, (CHUNKS - 1) * z_width], BF16)
+        halve(z_banks[0], z_bf[:, :z_width])
+        z_banks.append(psum.tile([P, SLABS, V_CHUNK], F32, name="z_bank3", tag="z_bank0"))
+        chunk_passes(z_banks[3], 3, 0, w1_mx0, picked0[1], range(SLABS))
+        chunk_passes(z_banks[3], 3, 1, w1_mx1, picked1[1], range(SLABS))
+        for c in range(1, CHUNKS - 1):
+            halve(z_banks[c], z_bf[:, c * z_width : (c + 1) * z_width])
+
+        w2_bf0_lo = cast_slabs("w2_bf0_lo", w2_rows0, 0, half_slabs, on_vector)
         w2_bf0_hi = cast_slabs("w2_bf0_hi", w2_rows0, half_slabs, SLABS, on_vector)
         w2_mx0 = mx_tiles("w2_0", H)
         quantize(w2_mx0, 0, half_h, w2_bf0_lo[:])
         quantize(w2_mx0, half_h, H, w2_bf0_hi[:])
-        e_bf0 = sbuf("e_bf0", [P, J * PACK], BF16)
-        cast_queries(e_bf0, e_rows0, 0, J, on_scalar)
-        e_mx0 = mx_tiles("e_0", J, reuse="w1_bf1_lo")
-        quantize(e_mx0, 0, J, e_bf0[:])
+        z_mx = mx_tiles("z", V)
+        quantize(z_mx, 0, V_HALF, z_bf[:, : 2 * z_width])
 
-        z_width = V_CHUNK * PACK
-        z_bf = sbuf("z_bf", [P, (CHUNKS - 1) * z_width], BF16, reuse="picked_scales")
-        for c in range(CHUNKS - 1):
-            halve(z_banks[c], z_bf[:, c * z_width : (c + 1) * z_width], False)
+        g_banks = [psum.tile([P, SLABS, Q_TILE], F32, name="g_bank%d" % qt) for qt in range(Q_TILES)]
+        tile_passes(g_banks[0], 0, w2_mx0, e_mx[0, 0], range(SLABS))
 
-        g_banks = []
-        for qt in range(Q_TILES):
-            g_banks.append(psum.tile([P, SLABS, Q_TILE], F32, name="g_bank%d" % qt, tag="z_bank%d" % (qt + 1)))
-            query_passes(g_banks[qt], qt, 0, w2_mx0, e_mx0)
+        w2_bf1_hi = cast_slabs("w2_bf1_hi", w2_rows1, half_slabs, SLABS, on_vector)
+        w2_bf1_lo = cast_slabs("w2_bf1_lo", w2_rows1, 0, half_slabs, on_scalar)
+        e_bf10 = cast_tile(1, 0, on_vector)
+        w2_mx1 = mx_tiles("w2_1", H)
+        quantize(w2_mx1, half_h, H, w2_bf1_hi[:])
+        quantize(e_mx[1, 0], 0, Q_TILE, e_bf10[:])
+        quantize(w2_mx1, 0, half_h, w2_bf1_lo[:])
+        tile_passes(g_banks[0], 1, w2_mx1, e_mx[1, 0], hi_first)
+        e_bf01 = cast_tile(0, 1, on_scalar)
+        quantize(e_mx[0, 1], 0, Q_TILE, e_bf01[:])
+        tile_passes(g_banks[1], 0, w2_mx0, e_mx[0, 1], range(SLABS))
 
-        w2_mx1 = weight_pass("w2_1", w2_rows1)
-        e_mx1 = mx_tiles("e_1", J)
-        for qt, copy, reuse in ((0, on_vector, None), (1, on_scalar, "picked1_0")):
-            e_bf1 = sbuf("e_bf1_%d" % qt, [P, Q_TILE * PACK], BF16, reuse)
-            cast_queries(e_bf1, e_rows1[:, :, qt * Q_TILE : (qt + 1) * Q_TILE], 0, Q_TILE, copy)
-            quantize(e_mx1, qt * Q_TILE, (qt + 1) * Q_TILE, e_bf1[:])
-            query_passes(g_banks[qt], qt, 1, w2_mx1, e_mx1)
+        e_mx[1, 1] = mx_tiles("e_1_1", Q_TILE)
+        e_bf11 = []
+        for half, copy in ((0, on_vector), (1, on_scalar)):
+            e_bf11.append(sbuf("e_bf1_1_%d" % half, [P, half_q * PACK], BF16))
+            cast_queries(e_bf11[half], e_rows[1, 1][:, :, half * half_q : (half + 1) * half_q], 0, half_q, copy)
+        for half in (1, 0):
+            quantize(e_mx[1, 1], half * half_q, (half + 1) * half_q, e_bf11[half][:])
+        tile_passes(g_banks[1], 1, w2_mx1, e_mx[1, 1], range(SLABS))
 
         z_bf3 = sbuf("z_bf3", [P, z_width], BF16, reuse="x_store0")
-        halve(z_banks[3], z_bf3[:], False)
-        z_mx = mx_tiles("z", V, reuse="picked1_0")
-        quantize(z_mx, 0, V_HALF, z_bf[:, : 2 * z_width])
+        halve(z_banks[3], z_bf3[:])
         quantize(z_mx, V_HALF, V - V_CHUNK, z_bf[:, 2 * z_width :])
         quantize(z_mx, V - V_CHUNK, V, z_bf3[:])
         g_mx = []

@@ -93,7 +93,7 @@ def tile_picked_zproto_none_p_kernel(tc, x_words, x_scales, w1, w2, eT, offs, ou
         offsets = sbuf("offsets", [P, S // 16], U16)
         scale_store = sbuf("scale_store", [P, T], U8)
         member_scales = sbuf("member_scales", [P, D, V], U8)
-        half_slabs, half_h, half_q = SLABS // 2, H // 2, Q_TILE // 2
+        half_slabs, half_h = SLABS // 2, H // 2
         lower, upper = range(half_slabs), range(half_slabs, SLABS)
 
         def move_scale_rows(o):
@@ -107,10 +107,10 @@ def tile_picked_zproto_none_p_kernel(tc, x_words, x_scales, w1, w2, eT, offs, ou
                 out=dst.rearrange("p (v t) -> p v t", t=SLABS), in_=bank[:].rearrange("p t v -> p v t"), func=ACT.Copy, scale=1.0 / D
             )
 
-        def tile_passes(bank, o, w2_mx, e_mx, slabs):
+        def tile_passes(bank, w2_mx, e_mx, slabs, opens=False, closes=False):
             for n, t in enumerate(slabs):
-                first = o == 0 and n == 0
-                last = o == PASSES - 1 and n == SLABS - 1
+                first = opens and n == 0
+                last = closes and n == len(slabs) - 1
                 multiply(bank[:, t, :], mx_columns(w2_mx, t * P, (t + 1) * P), mx_columns(e_mx, 0, Q_TILE), first, last)
 
         def chunk_passes(bank, c, o, w1_mx, words, slabs):
@@ -162,13 +162,14 @@ def tile_picked_zproto_none_p_kernel(tc, x_words, x_scales, w1, w2, eT, offs, ou
             chunk_passes(z_banks[c], c, 0, w1_mx0, picked0[c * V_CHUNK // V_HALF], range(SLABS))
         picked1 = [gather_words(x_store1, 1, half) for half in range(2)]
         w1_bf1_lo = cast_slabs("w1_bf1_lo", w1_rows1, 0, half_slabs, on_scalar)
-        w1_bf1_hi = cast_slabs("w1_bf1_hi", w1_rows1, half_slabs, SLABS, on_vector)
+        w1_bf1_third = cast_slabs("w1_bf1_third", w1_rows1, half_slabs, SLABS - 1, on_scalar)
         w1_mx1 = mx_tiles("w1_1", H)
-        quantize(w1_mx1, half_h, H, w1_bf1_hi[:])
         quantize(w1_mx1, 0, half_h, w1_bf1_lo[:])
-        hi_first = tuple(upper) + tuple(lower)
+        w1_bf1_last = cast_slabs("w1_bf1_last", w1_rows1, SLABS - 1, SLABS, on_vector, reuse="w1_bf1_lo")
+        quantize(w1_mx1, half_h, H - P, w1_bf1_third[:])
+        quantize(w1_mx1, H - P, H, w1_bf1_last[:])
         for c in range(CHUNKS - 1):
-            chunk_passes(z_banks[c], c, 1, w1_mx1, picked1[c * V_CHUNK // V_HALF], hi_first)
+            chunk_passes(z_banks[c], c, 1, w1_mx1, picked1[c * V_CHUNK // V_HALF], range(SLABS))
 
         e_mx = {}
 
@@ -183,23 +184,20 @@ def tile_picked_zproto_none_p_kernel(tc, x_words, x_scales, w1, w2, eT, offs, ou
 
         z_width = V_CHUNK * PACK
         z_bf = sbuf("z_bf", [P, (CHUNKS - 1) * z_width], BF16)
-        halve(z_banks[0], z_bf[:, :z_width])
-        z_banks.append(psum.tile([P, SLABS, V_CHUNK], F32, name="z_bank3", tag="z_bank0"))
+        for c in range(CHUNKS - 1):
+            halve(z_banks[c], z_bf[:, c * z_width : (c + 1) * z_width])
+        z_banks.append(psum.tile([P, SLABS, V_CHUNK], F32, name="z_bank3", tag="z_bank2"))
         chunk_passes(z_banks[3], 3, 0, w1_mx0, picked0[1], range(SLABS))
         chunk_passes(z_banks[3], 3, 1, w1_mx1, picked1[1], range(SLABS))
-        for c in range(1, CHUNKS - 1):
-            halve(z_banks[c], z_bf[:, c * z_width : (c + 1) * z_width])
 
         w2_bf0_lo = cast_slabs("w2_bf0_lo", w2_rows0, 0, half_slabs, on_vector)
         w2_bf0_hi = cast_slabs("w2_bf0_hi", w2_rows0, half_slabs, SLABS, on_vector)
         w2_mx0 = mx_tiles("w2_0", H)
         quantize(w2_mx0, 0, half_h, w2_bf0_lo[:])
         quantize(w2_mx0, half_h, H, w2_bf0_hi[:])
-        z_mx = mx_tiles("z", V)
-        quantize(z_mx, 0, V_HALF, z_bf[:, : 2 * z_width])
 
         g_banks = [psum.tile([P, SLABS, Q_TILE], F32, name="g_bank%d" % qt) for qt in range(Q_TILES)]
-        tile_passes(g_banks[0], 0, w2_mx0, e_mx[0, 0], range(SLABS))
+        tile_passes(g_banks[0], w2_mx0, e_mx[0, 0], range(SLABS), opens=True)
 
         w2_bf1_hi = cast_slabs("w2_bf1_hi", w2_rows1, half_slabs, SLABS, on_vector)
         w2_bf1_lo = cast_slabs("w2_bf1_lo", w2_rows1, 0, half_slabs, on_scalar)
@@ -208,23 +206,19 @@ def tile_picked_zproto_none_p_kernel(tc, x_words, x_scales, w1, w2, eT, offs, ou
         quantize(w2_mx1, half_h, H, w2_bf1_hi[:])
         quantize(e_mx[1, 0], 0, Q_TILE, e_bf10[:])
         quantize(w2_mx1, 0, half_h, w2_bf1_lo[:])
-        tile_passes(g_banks[0], 1, w2_mx1, e_mx[1, 0], hi_first)
+        tile_passes(g_banks[0], w2_mx1, e_mx[1, 0], tuple(upper) + tuple(lower), closes=True)
         e_bf01 = cast_tile(0, 1, on_scalar)
         quantize(e_mx[0, 1], 0, Q_TILE, e_bf01[:])
-        tile_passes(g_banks[1], 0, w2_mx0, e_mx[0, 1], range(SLABS))
+        tile_passes(g_banks[1], w2_mx0, e_mx[0, 1], range(SLABS), opens=True)
 
-        e_mx[1, 1] = mx_tiles("e_1_1", Q_TILE)
-        e_bf11 = []
-        for half, copy in ((0, on_vector), (1, on_scalar)):
-            e_bf11.append(sbuf("e_bf1_1_%d" % half, [P, half_q * PACK], BF16))
-            cast_queries(e_bf11[half], e_rows[1, 1][:, :, half * half_q : (half + 1) * half_q], 0, half_q, copy)
-        for half in (1, 0):
-            quantize(e_mx[1, 1], half * half_q, (half + 1) * half_q, e_bf11[half][:])
-        tile_passes(g_banks[1], 1, w2_mx1, e_mx[1, 1], range(SLABS))
+        e_bf11 = cast_tile(1, 1, on_vector)
+        quantize(e_mx[1, 1], 0, Q_TILE, e_bf11[:])
+        tile_passes(g_banks[1], w2_mx1, e_mx[1, 1], range(SLABS), closes=True)
 
-        z_bf3 = sbuf("z_bf3", [P, z_width], BF16, reuse="x_store0")
+        z_bf3 = sbuf("z_bf3", [P, z_width], BF16, reuse="w2_bf1_lo")
         halve(z_banks[3], z_bf3[:])
-        quantize(z_mx, V_HALF, V - V_CHUNK, z_bf[:, 2 * z_width :])
+        z_mx = mx_tiles("z", V, reuse="e_bf1_1")
+        quantize(z_mx, 0, V - V_CHUNK, z_bf[:])
         quantize(z_mx, V - V_CHUNK, V, z_bf3[:])
         g_mx = []
         for qt in range(Q_TILES):

@@ -39,7 +39,7 @@ def tile_picked_zproto_none_p_kernel(tc, x_words, x_scales, w1, w2, eT, offs, ou
         psum = ctx.enter_context(tc.psum_pool(name="psum", bufs=1))
 
         def sbuf(name, shape, dtype, reuse=None):
-            return keep.tile(shape, dtype, name=name, tag=reuse or name, align_bytes=64)
+            return keep.tile(shape, dtype, name=name, tag=reuse or name, align_bytes=256)
 
         def load_pass(dst, src, o):
             rows = dst.rearrange("p (j c) -> p j c", j=PACK)

@@ -96,8 +96,8 @@ def tile_picked_zproto_none_p_kernel(tc, x_words, x_scales, w1, w2, eT, offs, ou
         half_slabs, half_h = SLABS // 2, H // 2
         lower, upper = range(half_slabs), range(half_slabs, SLABS)
 
-        def move_scale_rows(o):
-            for r in range(1, SCALE_ROWS):
+        def move_scale_rows(r):
+            for o in range(PASSES):
                 nc.sync.dma_start(
                     out=scale_rows[SCALE_ROWS * o + r : P : QUADRANT, :], in_=scale_rows[SCALE_ROWS * o + 8 * r : P : QUADRANT, :]
                 )
@@ -137,8 +137,8 @@ def tile_picked_zproto_none_p_kernel(tc, x_words, x_scales, w1, w2, eT, offs, ou
         nc.vector.tensor_copy(out=picked_scales[:], in_=scale_store[:].indirect(offsets[:]))
         nc.vector.tensor_copy(out=member_scales[:], in_=picked_scales[:].rearrange("p (v d) -> p d v", d=D))
         scale_rows = member_scales[:].rearrange("p d v -> p (d v)").bitcast(I32)
-        move_scale_rows(0)
-        move_scale_rows(1)
+        for r in range(1, SCALE_ROWS):
+            move_scale_rows(r)
 
         picked0 = [gather_words(x_store0, 0, half) for half in range(2)]
         w_width, e_width = PACK * H, PACK * Q_TILE
@@ -162,14 +162,12 @@ def tile_picked_zproto_none_p_kernel(tc, x_words, x_scales, w1, w2, eT, offs, ou
             chunk_passes(z_banks[c], c, 0, w1_mx0, picked0[c * V_CHUNK // V_HALF], range(SLABS))
         picked1 = [gather_words(x_store1, 1, half) for half in range(2)]
         w1_bf1_lo = cast_slabs("w1_bf1_lo", w1_rows1, 0, half_slabs, on_scalar)
-        w1_bf1_third = cast_slabs("w1_bf1_third", w1_rows1, half_slabs, SLABS - 1, on_scalar)
+        w1_bf1_hi = cast_slabs("w1_bf1_hi", w1_rows1, half_slabs, SLABS, on_vector)
         w1_mx1 = mx_tiles("w1_1", H)
+        quantize(w1_mx1, half_h, H, w1_bf1_hi[:])
         quantize(w1_mx1, 0, half_h, w1_bf1_lo[:])
-        w1_bf1_last = cast_slabs("w1_bf1_last", w1_rows1, SLABS - 1, SLABS, on_vector, reuse="w1_bf1_lo")
-        quantize(w1_mx1, half_h, H - P, w1_bf1_third[:])
-        quantize(w1_mx1, H - P, H, w1_bf1_last[:])
         for c in range(CHUNKS - 1):
-            chunk_passes(z_banks[c], c, 1, w1_mx1, picked1[c * V_CHUNK // V_HALF], range(SLABS))
+            chunk_passes(z_banks[c], c, 1, w1_mx1, picked1[c * V_CHUNK // V_HALF], tuple(upper) + tuple(lower))
 
         e_mx = {}
 

@@ -213,7 +213,7 @@ def tile_picked_zproto_none_p_kernel(tc, x_words, x_scales, w1, w2, eT, offs, ou
         quantize(e_mx[1, 1], 0, Q_TILE, e_bf11[:])
         tile_passes(g_banks[1], w2_mx1, e_mx[1, 1], range(SLABS), closes=True)
 
-        z_bf3 = sbuf("z_bf3", [P, z_width], BF16, reuse="w2_bf1_lo")
+        z_bf3 = sbuf("z_bf3", [P, z_width], BF16, reuse="w2_bf1_hi")
         halve(z_banks[3], z_bf3[:])
         z_mx = mx_tiles("z", V, reuse="e_bf1_1")
         quantize(z_mx, 0, V - V_CHUNK, z_bf[:])

@@ -68,6 +68,12 @@ def tile_picked_zproto_none_p_kernel(tc, x_words, x_scales, w1, w2, eT, offs, ou
             )
             return grouped
 
+        def cast_slab_part(grouped, rows, t, u0, u1, copy):
+            copy(
+                out=grouped[:].rearrange("p (t u a j) -> p t u j a", u=P // RUN, a=RUN, j=PACK)[:, t, u0:u1],
+                in_=rows.rearrange("p j (u t a) -> p t u j a", t=SLABS, a=RUN)[:, t, u0:u1],
+            )
+
         def cast_queries(grouped, rows, c0, c1, copy):
             copy(
                 out=grouped[:, c0 * PACK : c1 * PACK].rearrange("p (c a j) -> p c j a", a=RUN, j=PACK),
@@ -142,17 +148,15 @@ def tile_picked_zproto_none_p_kernel(tc, x_words, x_scales, w1, w2, eT, offs, ou
 
         picked0 = [gather_words(x_store0, 0, half) for half in range(2)]
         w_width, e_width = PACK * H, PACK * Q_TILE
-        mid_raw = sbuf("mid_raw", [P, w_width + e_width], F32, reuse="picked_scales")
-        w1_rows1 = load_pass(mid_raw[:, :w_width], w1, 1)
+        w1_rows1 = load_pass(sbuf("w1_raw1", [P, w_width], F32, reuse="picked_scales")[:], w1, 1)
         e_rows = {}
-        e_rows[0, 0] = load_pass(mid_raw[:, w_width:], eT[:, :Q_TILE], 0)
         w1_bf0 = cast_slabs("w1_bf0", w1_rows0, 0, SLABS, on_scalar)
         w1_mx0 = mx_tiles("w1_0", H)
         quantize(w1_mx0, 0, H, w1_bf0[:])
-        last_raw = sbuf("last_raw", [P, 2 * w_width + 3 * e_width], F32, reuse="x_store0")
+        last_raw = sbuf("last_raw", [P, 2 * w_width + 4 * e_width], F32, reuse="x_store0")
         w2_rows0 = load_pass(last_raw[:, :w_width], w2, 0)
         w2_rows1 = load_pass(last_raw[:, w_width : 2 * w_width], w2, 1)
-        for n, (o, qt) in enumerate(((1, 0), (0, 1), (1, 1))):
+        for n, (o, qt) in enumerate(((1, 0), (0, 0), (0, 1), (1, 1))):
             c0 = 2 * w_width + n * e_width
             e_rows[o, qt] = load_pass(last_raw[:, c0 : c0 + e_width], eT[:, qt * Q_TILE : (qt + 1) * Q_TILE], o)
 
@@ -177,9 +181,6 @@ def tile_picked_zproto_none_p_kernel(tc, x_words, x_scales, w1, w2, eT, offs, ou
             e_mx[o, qt] = mx_tiles("e_%d_%d" % (o, qt), Q_TILE)
             return grouped
 
-        e_bf00 = cast_tile(0, 0, on_scalar)
-        quantize(e_mx[0, 0], 0, Q_TILE, e_bf00[:])
-
         z_width = V_CHUNK * PACK
         z_bf = sbuf("z_bf", [P, (CHUNKS - 1) * z_width], BF16)
         for c in range(CHUNKS - 1):
@@ -195,16 +196,22 @@ def tile_picked_zproto_none_p_kernel(tc, x_words, x_scales, w1, w2, eT, offs, ou
         quantize(w2_mx0, half_h, H, w2_bf0_hi[:])
 
         g_banks = [psum.tile([P, SLABS, Q_TILE], F32, name="g_bank%d" % qt) for qt in range(Q_TILES)]
-        tile_passes(g_banks[0], w2_mx0, e_mx[0, 0], range(SLABS), opens=True)
 
         w2_bf1_hi = cast_slabs("w2_bf1_hi", w2_rows1, half_slabs, SLABS, on_vector)
-        w2_bf1_lo = cast_slabs("w2_bf1_lo", w2_rows1, 0, half_slabs, on_scalar)
+        w2_bf1_lo = sbuf("w2_bf1_lo", [P, half_slabs * P * PACK], BF16)
+        runs = P // RUN
+        cast_slab_part(w2_bf1_lo, w2_rows1, 0, 0, runs, on_scalar)
+        cast_slab_part(w2_bf1_lo, w2_rows1, 1, 0, runs // 2, on_scalar)
+        cast_slab_part(w2_bf1_lo, w2_rows1, 1, runs // 2, runs, on_vector)
         e_bf10 = cast_tile(1, 0, on_vector)
         w2_mx1 = mx_tiles("w2_1", H)
         quantize(w2_mx1, half_h, H, w2_bf1_hi[:])
         quantize(e_mx[1, 0], 0, Q_TILE, e_bf10[:])
         quantize(w2_mx1, 0, half_h, w2_bf1_lo[:])
-        tile_passes(g_banks[0], w2_mx1, e_mx[1, 0], tuple(upper) + tuple(lower), closes=True)
+        tile_passes(g_banks[0], w2_mx1, e_mx[1, 0], tuple(upper) + tuple(lower), opens=True)
+        e_bf00 = cast_tile(0, 0, on_scalar)
+        quantize(e_mx[0, 0], 0, Q_TILE, e_bf00[:])
+        tile_passes(g_banks[0], w2_mx0, e_mx[0, 0], range(SLABS), closes=True)
         e_bf01 = cast_tile(0, 1, on_scalar)
         quantize(e_mx[0, 1], 0, Q_TILE, e_bf01[:])
         tile_passes(g_banks[1], w2_mx0, e_mx[0, 1], range(SLABS), opens=True)
@@ -213,7 +220,7 @@ def tile_picked_zproto_none_p_kernel(tc, x_words, x_scales, w1, w2, eT, offs, ou
         quantize(e_mx[1, 1], 0, Q_TILE, e_bf11[:])
         tile_passes(g_banks[1], w2_mx1, e_mx[1, 1], range(SLABS), closes=True)
 
-        z_bf3 = sbuf("z_bf3", [P, z_width], BF16, reuse="w2_bf1_hi")
+        z_bf3 = sbuf("z_bf3", [P, z_width], BF16, reuse="e_bf0_0")
         halve(z_banks[3], z_bf3[:])
         z_mx = mx_tiles("z", V, reuse="e_bf1_1")
         quantize(z_mx, 0, V - V_CHUNK, z_bf[:])

@@ -255,7 +255,11 @@ def tile_picked_zproto_none_p_kernel(tc, x_words, x_scales, w1, w2, eT, offs, ou
             nc.vector.tensor_scalar(out=prob[:], in0=exps[qt][:, :width], scalar1=inverse[:], scalar2=None, op0=ALU.mult)
             nc.sync.dma_start(out=out[qt * Q_TILE : (qt + 1) * Q_TILE, :width], in_=prob[:])
 
-        normalise_on_vector(0, V, inverse_total(0))
+        first_inverse = inverse_total(0)
+        first_prob = sbuf("prob0", [P, V], F32)
+        nc.vector.tensor_scalar(out=first_prob[:], in0=exps[0][:], scalar1=first_inverse[:], scalar2=None, op0=ALU.mult)
+        for parity, queue in enumerate((nc.sync, nc.scalar)):
+            queue.dma_start(out=out[parity:Q_TILE:2, :], in_=first_prob[parity:P:2, :])
         last_inverse = inverse_total(1)
         normalise_on_vector(1, V_HALF, last_inverse)
         prob_hi = sbuf("prob_hi", [P, V_HALF], F32)

from contextlib import ExitStack

import concourse.mybir as mybir

K, T, S, D, H, J, V = 1024, 4096, 1024, 2, 512, 256, 512
FLOPS = 2 * K * H * S + 2 * K * H * J + 2 * H * J * V

F32 = mybir.dt.float32
BF16 = mybir.dt.bfloat16
I32 = mybir.dt.int32
U32 = mybir.dt.uint32
U16 = mybir.dt.uint16
U8 = mybir.dt.uint8
FP8X4 = mybir.dt.float8_e4m3fn_x4
ACT = mybir.ActivationFunctionType
ALU = mybir.AluOpType

P = 128
PACK = 4
K_PASS = P * PACK
PASSES = K // K_PASS
SLABS = H // P
RUN = 4
QUADRANT = 32
SCALE_ROWS = 4
V_HALF = V // 2
V_CHUNK = 128
CHUNKS = V // V_CHUNK
Q_TILE = 128
Q_TILES = J // Q_TILE


def tile_picked_zproto_none_p_kernel(tc, x_words, x_scales, w1, w2, eT, offs, out):
    nc = tc.nc
    on_vector, on_scalar = nc.vector.tensor_copy, nc.scalar.copy

    with ExitStack() as ctx:
        keep = ctx.enter_context(tc.tile_pool(name="keep", bufs=1))
        psum = ctx.enter_context(tc.psum_pool(name="psum", bufs=1))

        def sbuf(name, shape, dtype, reuse=None):
            return keep.tile(shape, dtype, name=name, tag=reuse or name, align_bytes=256)

        def load_pass(dst, src, o):
            rows = dst.rearrange("p (j c) -> p j c", j=PACK)
            nc.sync.dma_start(out=rows, in_=src[o * K_PASS : (o + 1) * K_PASS, :].rearrange("(p j) c -> p j c", j=PACK))
            return rows

        def load_words(o, reuse=None):
            store = sbuf("x_store%d" % o, [P, T], I32, reuse)
            nc.sync.dma_start(out=store[:], in_=x_words[o].rearrange("p n r -> p (n r)").bitcast(I32))
            return store

        def gather_words(store, o, half):
            words = sbuf("picked%d_%d" % (o, half), [P, D, V_HALF], U32)
            columns = D * V_HALF // 16
            nc.vector.tensor_copy(
                out=words[:].rearrange("p d v -> p v d"),
                in_=store[:].bitcast(U32).indirect(offsets[:, half * columns : (half + 1) * columns]),
            )
            return words

        def cast_slabs(name, rows, t0, t1, copy, reuse=None):
            grouped = sbuf(name, [P, (t1 - t0) * P * PACK], BF16, reuse)
            copy(
                out=grouped[:].rearrange("p (t u a j) -> p u t j a", t=t1 - t0, a=RUN, j=PACK),
                in_=rows.rearrange("p j (u t a) -> p u t j a", t=SLABS, a=RUN)[:, :, t0:t1],
            )
            return grouped

        def cast_slab_part(grouped, rows, t, u0, u1, copy):
            copy(
                out=grouped[:].rearrange("p (t u a j) -> p t u j a", u=P // RUN, a=RUN, j=PACK)[:, t, u0:u1],
                in_=rows.rearrange("p j (u t a) -> p t u j a", t=SLABS, a=RUN)[:, t, u0:u1],
            )

        def cast_queries(grouped, rows, c0, c1, copy):
            copy(
                out=grouped[:, c0 * PACK : c1 * PACK].rearrange("p (c a j) -> p c j a", a=RUN, j=PACK),
                in_=rows[:, :, c0:c1].rearrange("p j (c a) -> p c j a", a=RUN),
            )

        def mx_tiles(name, width, reuse=None):
            return sbuf(name + "_codes", [P, width], U32, reuse), sbuf(name + "_scales", [P, width], U8)

        def mx_columns(mx, c0, c1):
            codes, scales = mx
            return codes[:, c0:c1].bitcast(FP8X4), scales[:, c0:c1]

        def quantize(mx, c0, c1, grouped):
            codes, scales = mx_columns(mx, c0, c1)
            nc.vector.quantize_mx(out=codes, scales=scales, in_=grouped)

        def multiply(dst, stationary, moving, start, stop):
            nc.tensor.matmul_mx(
                out=dst, lhsT=stationary[0], lhsT_scale=stationary[1], rhs=moving[0], rhs_scale=moving[1], start=start, stop=stop
            )

        offsets = sbuf("offsets", [P, S // 16], U16)
        scale_store = sbuf("scale_store", [P, T], U8)
        member_scales = sbuf("member_scales", [P, D, V], U8)
        half_slabs, half_h = SLABS // 2, H // 2
        lower, upper = range(half_slabs), range(half_slabs, SLABS)

        def move_scale_rows(r):
            for o in range(PASSES):
                nc.sync.dma_start(
                    out=scale_rows[SCALE_ROWS * o + r : P : QUADRANT, :], in_=scale_rows[SCALE_ROWS * o + 8 * r : P : QUADRANT, :]
                )

        def halve(bank, dst):
            nc.scalar.activation(
                out=dst.rearrange("p (v t) -> p v t", t=SLABS), in_=bank[:].rearrange("p t v -> p v t"), func=ACT.Copy, scale=1.0 / D
            )

        def tile_passes(bank, w2_mx, e_mx, slabs, opens=False, closes=False):
            for n, t in enumerate(slabs):
                first = opens and n == 0
                last = closes and n == len(slabs) - 1
                multiply(bank[:, t, :], mx_columns(w2_mx, t * P, (t + 1) * P), mx_columns(e_mx, 0, Q_TILE), first, last)

        def chunk_passes(bank, c, o, w1_mx, words, slabs):
            v0 = c * V_CHUNK
            v_in = v0 % V_HALF
            for n, t in enumerate(slabs):
                for d in range(D):
                    moving = (
                        words[:, d, v_in : v_in + V_CHUNK].bitcast(FP8X4),
                        member_scales[SCALE_ROWS * o : P, d, v0 : v0 + V_CHUNK],
                    )
                    first = o == 0 and n == 0 and d == 0
                    last = o == PASSES - 1 and n == SLABS - 1 and d == D - 1
                    multiply(bank[:, t, :], mx_columns(w1_mx, t * P, (t + 1) * P), moving, first, last)

        w1_rows0 = load_pass(sbuf("w1_raw0", [P, PACK * H], F32)[:], w1, 0)
        nc.sync.dma_start(offsets[:], offs)
        nc.vector.memset(scale_store[:].bitcast(I32), 0)
        nc.sync.dma_start(out=scale_store[0:P:4, :].bitcast(I32), in_=x_scales.rearrange("o m c -> m o c").bitcast(I32))
        x_store0 = load_words(0)
        x_store1 = load_words(1)

        picked_scales = sbuf("picked_scales", [P, S], U8)
        nc.vector.tensor_copy(out=picked_scales[:], in_=scale_store[:].indirect(offsets[:]))
        nc.vector.tensor_copy(out=member_scales[:], in_=picked_scales[:].rearrange("p (v d) -> p d v", d=D))
        scale_rows = member_scales[:].rearrange("p d v -> p (d v)").bitcast(I32)
        for r in range(1, SCALE_ROWS):
            move_scale_rows(r)

        picked0 = [gather_words(x_store0, 0, half) for half in range(2)]
        w_width, e_width = PACK * H, PACK * Q_TILE
        w1_rows1 = load_pass(sbuf("w1_raw1", [P, w_width], F32, reuse="picked_scales")[:], w1, 1)
        e_rows = {}
        w1_bf0 = cast_slabs("w1_bf0", w1_rows0, 0, SLABS, on_scalar)
        w1_mx0 = mx_tiles("w1_0", H)
        quantize(w1_mx0, 0, H, w1_bf0[:])
        last_raw = sbuf("last_raw", [P, 2 * w_width + 4 * e_width], F32, reuse="x_store0")
        w2_rows0 = load_pass(last_raw[:, :w_width], w2, 0)
        w2_rows1 = load_pass(last_raw[:, w_width : 2 * w_width], w2, 1)
        for n, (o, qt) in enumerate(((1, 0), (0, 0), (0, 1), (1, 1))):
            c0 = 2 * w_width + n * e_width
            e_rows[o, qt] = load_pass(last_raw[:, c0 : c0 + e_width], eT[:, qt * Q_TILE : (qt + 1) * Q_TILE], o)

        z_banks = []
        for c in range(CHUNKS - 1):
            z_banks.append(psum.tile([P, SLABS, V_CHUNK], F32, name="z_bank%d" % c, tag="z_bank%d" % c))
            chunk_passes(z_banks[c], c, 0, w1_mx0, picked0[c * V_CHUNK // V_HALF], range(SLABS))
        picked1 = [gather_words(x_store1, 1, half) for half in range(2)]
        w1_bf1_lo = cast_slabs("w1_bf1_lo", w1_rows1, 0, half_slabs, on_scalar)
        w1_bf1_hi = cast_slabs("w1_bf1_hi", w1_rows1, half_slabs, SLABS, on_vector)
        w1_mx1 = mx_tiles("w1_1", H)
        quantize(w1_mx1, half_h, H, w1_bf1_hi[:])
        quantize(w1_mx1, 0, half_h, w1_bf1_lo[:])
        for c in range(CHUNKS - 1):
            chunk_passes(z_banks[c], c, 1, w1_mx1, picked1[c * V_CHUNK // V_HALF], tuple(upper) + tuple(lower))

        e_mx = {}

        def cast_tile(o, qt, copy):
            grouped = sbuf("e_bf%d_%d" % (o, qt), [P, e_width], BF16)
            cast_queries(grouped, e_rows[o, qt], 0, Q_TILE, copy)
            e_mx[o, qt] = mx_tiles("e_%d_%d" % (o, qt), Q_TILE)
            return grouped

        z_width = V_CHUNK * PACK
        z_bf = sbuf("z_bf", [P, (CHUNKS - 1) * z_width], BF16)
        for c in range(CHUNKS - 1):
            halve(z_banks[c], z_bf[:, c * z_width : (c + 1) * z_width])
        z_banks.append(psum.tile([P, SLABS, V_CHUNK], F32, name="z_bank3", tag="z_bank2"))
        chunk_passes(z_banks[3], 3, 0, w1_mx0, picked0[1], range(SLABS))
        chunk_passes(z_banks[3], 3, 1, w1_mx1, picked1[1], range(SLABS))

        w2_bf0_lo = cast_slabs("w2_bf0_lo", w2_rows0, 0, half_slabs, on_vector)
        w2_bf0_hi = cast_slabs("w2_bf0_hi", w2_rows0, half_slabs, SLABS, on_vector)
        w2_mx0 = mx_tiles("w2_0", H)
        quantize(w2_mx0, 0, half_h, w2_bf0_lo[:])
        quantize(w2_mx0, half_h, H, w2_bf0_hi[:])

        g_banks = [psum.tile([P, SLABS, Q_TILE], F32, name="g_bank%d" % qt) for qt in range(Q_TILES)]

        w2_bf1_hi = cast_slabs("w2_bf1_hi", w2_rows1, half_slabs, SLABS, on_vector)
        w2_bf1_lo = sbuf("w2_bf1_lo", [P, half_slabs * P * PACK], BF16)
        runs = P // RUN
        cast_slab_part(w2_bf1_lo, w2_rows1, 0, 0, runs, on_scalar)
        cast_slab_part(w2_bf1_lo, w2_rows1, 1, 0, runs // 2, on_scalar)
        cast_slab_part(w2_bf1_lo, w2_rows1, 1, runs // 2, runs, on_vector)
        e_bf10 = cast_tile(1, 0, on_vector)
        w2_mx1 = mx_tiles("w2_1", H)
        quantize(w2_mx1, half_h, H, w2_bf1_hi[:])
        quantize(e_mx[1, 0], 0, Q_TILE, e_bf10[:])
        quantize(w2_mx1, 0, half_h, w2_bf1_lo[:])
        tile_passes(g_banks[0], w2_mx1, e_mx[1, 0], tuple(upper) + tuple(lower), opens=True)
        e_bf00 = cast_tile(0, 0, on_scalar)
        quantize(e_mx[0, 0], 0, Q_TILE, e_bf00[:])
        tile_passes(g_banks[0], w2_mx0, e_mx[0, 0], range(SLABS), closes=True)
        e_bf01 = cast_tile(0, 1, on_scalar)
        quantize(e_mx[0, 1], 0, Q_TILE, e_bf01[:])
        tile_passes(g_banks[1], w2_mx0, e_mx[0, 1], range(SLABS), opens=True)

        e_bf11 = cast_tile(1, 1, on_vector)
        quantize(e_mx[1, 1], 0, Q_TILE, e_bf11[:])
        tile_passes(g_banks[1], w2_mx1, e_mx[1, 1], range(SLABS), closes=True)

        z_bf3 = sbuf("z_bf3", [P, z_width], BF16, reuse="e_bf0_0")
        halve(z_banks[3], z_bf3[:])
        z_mx = mx_tiles("z", V, reuse="e_bf1_1")
        quantize(z_mx, 0, V - V_CHUNK, z_bf[:])
        quantize(z_mx, V - V_CHUNK, V, z_bf3[:])
        g_mx = []
        for qt in range(Q_TILES):
            g_bf = sbuf("g_bf%d" % qt, [P, Q_TILE * PACK], BF16)
            on_scalar(out=g_bf[:].rearrange("p (q t) -> p q t", t=SLABS), in_=g_banks[qt][:].rearrange("p t q -> p q t"))
            g_mx.append(mx_tiles("g_%d" % qt, Q_TILE))
            quantize(g_mx[qt], 0, Q_TILE, g_bf[:])

        y_banks = []
        for qt in range(Q_TILES):
            y_banks.append(psum.tile([P, V], F32, name="y_bank%d" % qt))
            multiply(y_banks[qt][:], mx_columns(g_mx[qt], 0, Q_TILE), mx_columns(z_mx, 0, V), True, True)
        neg_max, exps, totals = [], [], []
        for qt in range(Q_TILES):
            neg_max.append(sbuf("neg_max%d" % qt, [P, 1], F32))
            nc.vector.tensor_reduce(out=neg_max[qt][:], in_=y_banks[qt][:], axis=mybir.AxisListType.X, op=ALU.max, negate=True)
        for qt in range(Q_TILES):
            exps.append(sbuf("exp%d" % qt, [P, V], F32))
            totals.append(sbuf("total%d" % qt, [P, 1], F32))
            nc.scalar.activation(out=exps[qt][:], in_=y_banks[qt][:], func=ACT.Exp, bias=neg_max[qt][:], accum_out=totals[qt][:])

        def inverse_total(qt):
            inverse = sbuf("inverse%d" % qt, [P, 1], F32)
            nc.vector.reciprocal(out=inverse[:], in_=totals[qt][:])
            return inverse

        def normalise_on_vector(qt, width, inverse):
            prob = sbuf("prob%d" % qt, [P, width], F32)
            nc.vector.tensor_scalar(out=prob[:], in0=exps[qt][:, :width], scalar1=inverse[:], scalar2=None, op0=ALU.mult)
            nc.sync.dma_start(out=out[qt * Q_TILE : (qt + 1) * Q_TILE, :width], in_=prob[:])

        first_inverse = inverse_total(0)
        first_prob = sbuf("prob0", [P, V], F32)
        nc.vector.tensor_scalar(out=first_prob[:], in0=exps[0][:], scalar1=first_inverse[:], scalar2=None, op0=ALU.mult)
        for parity, queue in enumerate((nc.sync, nc.scalar)):
            queue.dma_start(out=out[parity:Q_TILE:2, :], in_=first_prob[parity:P:2, :])
        last_inverse = inverse_total(1)
        normalise_on_vector(1, V_HALF, last_inverse)
        prob_hi = sbuf("prob_hi", [P, V_HALF], F32)
        nc.scalar.activation(out=prob_hi[:], in_=exps[1][:, V_HALF:], func=ACT.Copy, scale=last_inverse[:])
        nc.scalar.dma_start(out=out[Q_TILE:, V_HALF:], in_=prob_hi[:])
